import numpy as np, ml_dtypes
CORES = [48,51,52,55]
N = 4
import mx_ref
BF = ml_dtypes.bfloat16
def gentries(a):
    return np.ascontiguousarray(a.reshape(8, 16, -1).transpose(0, 2, 1)).reshape(8, -1)
def gtable(e):
    e = np.asarray(e); return np.ascontiguousarray(e.reshape(8, -1, 16).transpose(0, 2, 1)).reshape(128, -1).astype(np.int32)
def gcols(t, e):
    v = np.concatenate([t.reshape(8, 16, -1, 4), np.zeros((8, 16, 1, 4), BF)], axis=2)
    return np.ascontiguousarray(np.stack([v[g][:, e[g]] for g in range(8)])).reshape(128, -1)
def tile(rs):
    return np.stack(rs, axis=2).reshape(128, -1).astype(BF)
def pick(q, e):
    c = np.concatenate([q[0].reshape(128, -1, 4), np.zeros((128, 1, 4), np.uint8)], axis=1); s = np.concatenate([q[1], np.ones((16, 1), np.uint8)], axis=1)
    return (np.ascontiguousarray(c[:, e].reshape(128, -1)), np.ascontiguousarray(s[:, e]))
def join(*qs):
    return (np.concatenate([q[0] for q in qs], axis=1), np.concatenate([q[1] for q in qs], axis=1))
def put(q, e, v):
    c, s = q[0].reshape(128, -1, 4).copy(), q[1].copy(); c[:, e] = v[0].reshape(128, -1, 4); s[:, e] = v[1]
    return (c.reshape(128, -1), s)
def pk(c, s):
    return (np.ascontiguousarray(c), mx_ref.live(s))
def emit(q):
    return q[0], q[1]
def packed(v, rng):
    q = [mx_ref.quantize(np.ascontiguousarray(v[r])) for r in range(N)]
    return np.stack([a for a, b in q]), np.stack([mx_ref.plane(b, rng) for a, b in q])
def values_of_codes():
    e, c = np.zeros((128, 128, 4), np.float32), np.zeros((128, 2, 4), np.uint8)
    e[np.arange(128), np.arange(128), 0] = 1
    c[:127, :, 0] = np.arange(256).reshape(2, 128).T[:127]
    return mx_ref.matmul(mx_ref.quantize(e.reshape(128, 512).astype(BF)), (c.reshape(128, 8), np.full((16, 2), 127, np.uint8))).T.reshape(-1).astype(np.float64)
CODE_VALUE, SCALE_VALUE = values_of_codes(), 2.0 ** (np.arange(256) - 127.0)
def decode(q):
    return (CODE_VALUE[q[0]].reshape(16, 8, -1, 4) * SCALE_VALUE[q[1]][:, None, :, None] + 0.0).reshape(128, -1).astype(np.float32)
def f(rng, *shape):
    return mx_ref.flush((rng.standard_normal(shape, dtype=np.float32) * np.exp2(rng.integers(-2, 3, shape[:-1] + (1,)))).astype(BF))
def wide(rng, *shape, cols=0):
    v = rng.standard_normal(shape, dtype=np.float32) * np.exp2(rng.integers(-12, 13, shape)).astype(np.float32)
    if cols: v *= np.repeat(np.exp2(rng.integers(-cols, cols + 1, shape[:-2] + (1, shape[-1] // 4))) * (rng.random(shape[:-2] + (1, shape[-1] // 4)) > 0.0625), 4, axis=-1).astype(np.float32)
    return mx_ref.flush(v.astype(BF))
C, L, M, R = 448, 64, 224, 3
STEP = [1, 2, 3]
place = np.arange(C)
def at(a, e):
    return np.take_along_axis(a, e, axis=1)
def big(v):
    v = v.astype(np.float32)
    v[np.abs(v) < np.float32(2.0 ** -16)] = 0
    return v.astype(BF)
def numbers_of(rng):
    return {"x": big(f(rng, N, 128, 4 * C)), "u": np.array(f(rng, N, 128, 512)), "v": np.array(f(rng, N, 128, 512))}
def layers(rng):
    return big(f(rng, N, 128, 2048)).reshape(N, 8, 16, 4, 8, 16, 4)
def weights(rng, w):
    c, p = packed(np.ascontiguousarray(w).reshape(N, 128, 2048), rng)
    return {"wc": c, "ws": p}
def twins(rng):
    o = np.argsort(rng.random((N, 8, C)), axis=2)
    e = np.zeros((N, 8, C), int)
    np.put_along_axis(e, o[:, :, :M], o[:, :, M:], axis=2)
    np.put_along_axis(e, o[:, :, M:], o[:, :, :M], axis=2)
    return e
def listed(e):
    return {"tw": np.stack([gtable(e[r]) for r in range(N)])}
def signs(rng):
    return np.stack([rng.permutation(8) % 2 * 2.0 - 1.0 for r in range(N)])
def setup_inputs(rng):
    return {**numbers_of(rng), **weights(rng, layers(rng)), **listed(twins(rng))}
def setup_inputs_ties(rng):
    d = numbers_of(rng)
    e = rng.permutation(N)
    x = d["x"].reshape(N, 8, 16, C, 4)
    for r in range(N):
        k = np.zeros(C, int) if r == e[0] else rng.permutation(C) % 3
        a = x[r][:, :8, :3].copy()
        a[:, :, 2] = 0
        x[r][:, :8] = a[:, :, k]
    x[e[1]] = 0
    u = d["u"].reshape(N, 8, 16, 8, 16, 4)
    k = u.copy()
    u[:, :, :, :, 0] = 0
    for g in range(8): u[:, g, :8, g, 0] = k[:, g, :8, g, 0]
    w = layers(rng)
    w[:, :, :, :, :, :8] = 0
    return {"x": x.reshape(N, 128, 4 * C), "u": u.reshape(N, 128, 512), "v": d["v"], **weights(rng, w), **listed(twins(rng))}
def setup_inputs_near(rng):
    d = numbers_of(rng)
    x = np.zeros((N, 8, 16, C, 4), np.float32)
    u = d["u"].reshape(N, 128, 128, 4)
    u[:, :, ::16] = 0
    o, e = rng.permutation(N) % 4, twins(rng)
    n = np.arange(M)
    for r in range(N):
        size = 1.0 if o[r] < 2 else 2.0 ** -4
        k = 1.0 if o[r] == 0 else 2.0 ** -30
        kind = rng.permutation(8)
        for g in range(8):
            low = np.flatnonzero(place < e[r, g])
            high = e[r, g][low]
            h, c = 16 * g, 1.0 - 2.0 * (kind[g] % 2)
            u[r, h, h, 0] = k
            u[r, h + 8:h + 12, h] = k
            s, unit = np.zeros(C, int), 2.0 ** -23 * size
            if kind[g] < 4:
                i = (n + rng.integers(0, (M - L) // 2 + 1)) % M
                upper = i // (M // 2)
                more = (M - i) // 2 + 1 if o[r] < 2 else M // 2 - i % (M // 2) + 1 - upper
                s[low] = rng.integers(0, 255 - M // 2, M)
                s[high] = s[low] + more
                if o[r] < 2:
                    u[r, h, h, 0] = k * 2.0 ** 20
                    x[r, g, 0, :, 0] = c * 2.0 ** -20
                    j = int(np.argmax(more))
                    if kind[g] < 2: x[r, g, 0, high[j] if c > 0 else low[j], 0] *= np.float32(2.0 ** 50)
                else:
                    x[r, g, 0, :, 0] = 8 * 2.0 ** -30
                    x[r, g, 0, high[upper == 0], 0] = 9 * 2.0 ** -30
            elif o[r] < 2:
                great, small = (high, low) if c > 0 else (low, high)
                third = 3 * n // M
                s[small] = 512 * (2 * int(rng.integers(17, 32)) - (third == 0)) + 255 * (third != 1)
                x[r, g, 0, great, 0] = 512 * c
                x[r, g, 0, small, 0] = 0.5 * c
                unit = 2.0 ** -24 * c
            else:
                m = np.where(n < M // 2, 10, 9) * 2.0 ** -32
                x[r, g, :2, :, 0] = 8 * 2.0 ** -32
                x[r, g, 0, high, 0] = m
                x[r, g, 1, low, 0] = m
                u[r, h, h, 0] = 9 * 2.0 ** -33
                u[r, h + 1, h, 0] = 2.0 ** -30
            z = ((s[:, None] >> np.arange(16)) & 1) * np.exp2(np.arange(16.0)) * unit + 0.0
            for i in range(4): x[r, g, 8 + i] = z[:, 4 * i:4 * i + 4]
        x[r, :, 12:] = rng.integers(4, 8, (8, 4, C, 4)) * 2.0 ** -20 * size
    w = layers(rng)
    w[:, :, :12] = 0
    w[:, :, :, :, :, :12] = 0
    return {"x": x.reshape(N, 128, 4 * C).astype(BF), "u": u.reshape(N, 128, 512), "v": d["v"], **weights(rng, w), **listed(e)}
def setup_inputs_arcs(rng):
    d = numbers_of(rng)
    x = d["x"].astype(np.float32).reshape(N, 8, 16, C, 4)
    u = d["u"].reshape(N, 128, 128, 4)
    u[:, :, ::16] = 0
    size = np.where(rng.permutation(N) < N // 2, 2.0 ** -30, 1.0).astype(np.float32).astype(BF)
    e = np.zeros((N, 8, C), int)
    for r in range(N):
        k, m, n = rng.permutation(8), rng.permutation(8), rng.permutation(8)
        for g in range(8):
            ways = [place, place[::-1], np.argsort(place % 2, kind="stable"), np.argsort(-(place % 2), kind="stable"), np.roll(place, M // 2), np.roll(place, int(rng.integers(1, C))), rng.permutation(C), rng.permutation(C)]
            low = np.sort(ways[k[g]][:M])
            high = np.setdiff1d(place, low)
            if m[g] % 3 == 1: high = high[::-1]
            if m[g] % 3 == 2: high = rng.permutation(high)
            more = [np.arange(1, M + 1), np.arange(M, 0, -1), np.ones(M, int), rng.permutation(M) + 1][n[g] % 4]
            key = np.zeros(C, int)
            key[low] = rng.integers(0, 256, M)
            key[high] = key[low] + more
            z = ((key[:, None] >> np.arange(12)) & 1) * np.exp2(np.arange(12.0))
            for i in range(3): x[r, g, 8 + i] = z[:, 4 * i:4 * i + 4]
            e[r, g, low] = high
            e[r, g, high] = low
        for h in range(0, 128, 16): u[r, h + 8:h + 11, h] = size[r]
    w = layers(rng)
    w[:, :, 8:11] = 0
    w[:, :, :, :, :, 8:11] = 0
    return {"x": x.reshape(N, 128, 4 * C).astype(BF), "u": u.reshape(N, 128, 512), "v": d["v"], **weights(rng, w), **listed(e)}
def setup_inputs_huge(rng):
    d = numbers_of(rng)
    e = twins(rng)
    c = np.ones((N, C))
    x = 0.7 + 0.2 * rng.random((N, 128, C, 4))
    a = 1 - 0.1 * rng.random((N, 128, 8, 4))
    for r in rng.permutation(N)[:N // 2]:
        x[r] = 0.9375 - 0.1 * rng.random((128, C, 4)) ** 4
        a[r] = 1 - 0.025 * rng.random((128, 8, 4))
        a[r, :, :, 0] = 1
        c[r] = rng.permutation(C) % 2 * 2.0 - 1.0
        for g in range(8):
            i, j = rng.permutation(np.flatnonzero(c[r] > 0)), np.flatnonzero(c[r] < 0)
            e[r, g, i] = j
            e[r, g, j] = i
    x = 2.0 ** 30 * x * c[:, None, :, None]
    u = d["u"].reshape(N, 128, 128, 4)
    a = 2.0 ** 30 * a * signs(rng)[:, None, :, None]
    u[:, :, ::16] = a.astype(np.float32).astype(BF)
    w = np.zeros((N, 128, 4, 128, 4), np.float32)
    i = np.arange(128)
    for b in range(4): w[:, i, b, i, b] = -0.25
    return {"x": x.astype(np.float32).reshape(N, 128, 4 * C).astype(BF), "u": u.reshape(N, 128, 512), "v": d["v"], **weights(rng, w.astype(BF)), **listed(e)}
def setup_inputs_spread(rng):
    d = setup_inputs(rng)
    d["x"] = big(wide(rng, N, 128, 4 * C, cols=6))
    return d
def check_inputs(d):
    b = []
    for k in ("x", "u", "v"):
        a = np.abs(d[k].astype(np.float32))
        if not (np.isfinite(a).all() and ((a == 0) | (a >= 2.0 ** -30) & (a <= 2.0 ** 30)).all()): b.append("a value of " + k)
    none, least, most = [emit(mx_ref.quantize(np.full((128, 16), k, np.float32).astype(BF)))[1][0, 0] for k in (0.0, 2.0 ** -30, 2.0 ** 30)]
    for r in range(N):
        if ((d["wc"][r] == 0x7F) | (d["wc"][r] == 0xFF)).any(): b.append("wc: a code that is no number")
        s = mx_ref.live(d["ws"][r])
        if ((s != none) & ((s < least) | (s > most))).any(): b.append("ws: a scale out of range")
        e = gentries(d["tw"][r])
        if ((e < 0) | (e >= C)).any(): b.append("tw: a twin out of range")
        elif (e == place).any() or (at(e, e) != place).any(): b.append("tw: places that aren't each other's twins")
    return b
def reference(x, u, v, wc, ws, tw):
    qu = [mx_ref.quantize(u[r]) for r in range(N)]
    lay = [pk(wc[r], ws[r]) for r in range(N)]
    now = [x[r] for r in range(N)]
    twin = [gentries(tw[r]) for r in range(N)]
    for t in range(R):
        kept, sent, named = [], [], []
        for r in range(N):
            e = twin[r]
            s = mx_ref.matmul(qu[r], mx_ref.quantize(now[r]))[::16] + np.float32(0.0)
            o = np.argsort(~((s < at(s, e)) | (s == at(s, e)) & (place > e)), axis=1, kind="stable")[:, :M]
            a = (np.stack([np.searchsorted(o[g], place, "right") for g in range(8)]) - 1) % M
            over = at(e, o)
            z = ((gcols(now[r], np.roll(o, 1, axis=1)).astype(np.float32) + gcols(now[r], at(o, at(a, over))).astype(np.float32)) * np.float32(0.5)).astype(BF)
            q = mx_ref.quantize(z)
            h = tile([mx_ref.matmul(pick(lay[r], np.arange(128 * b, 128 * b + 128)), q) * np.float32(0.03125) for b in range(4)])
            new = (now[r].astype(np.float32) + gcols(h, a).astype(np.float32)).astype(BF)
            weak = np.argsort(at(s, over) - at(s, o), axis=1, kind="stable")[:, :L]
            gone = np.zeros((8, C), bool)
            np.put_along_axis(gone, np.concatenate([at(o, weak), at(over, weak)], axis=1), True, axis=1)
            i = np.argsort(gone, axis=1, kind="stable")
            named.append(at(np.argsort(i, axis=1), at(e, i)))
            kept.append(gcols(new, i[:, :C - 2 * L]))
            sent.append(gcols(decode(mx_ref.quantize(new)).astype(BF), i[:, C - 2 * L:]))
        for r in range(N):
            p = (r - STEP[t]) % N
            now[r] = np.concatenate([kept[r], sent[p]], axis=1)
            twin[r] = np.concatenate([named[r][:, :C - 2 * L], named[p][:, C - 2 * L:]], axis=1)
    y, ot = np.zeros((N, 128, C), np.float32), np.zeros((N, 8, C), np.float32)
    oc, osc = np.zeros((N, 128, 4 * C), np.uint8), np.zeros((N, 16, C), np.uint8)
    for r in range(N):
        q = mx_ref.quantize(now[r])
        y[r] = mx_ref.matmul(mx_ref.quantize(v[r]), q)
        ot[r] = twin[r]
        oc[r], osc[r] = emit(q)
    return {"y": y, "ot": ot, "oc": oc, "osc": osc}

@@ -1,0 +1,522 @@
+from concourse.mybir import dt, AluOpType as ALU, AxisListType as AX, ActivationFunctionType as AF
+
+C, M, LV2, ST, R = 448, 224, 128, 320, 3
+STEP = (1, 2, 3)
+PW = 240
+UW = 256
+C2 = 2 * C
+BIG = 2.0 ** 21
+HUGE = 2.0 ** 80
+TINY = 2.0 ** -120
+BY_SCAN = (2, 3)
+F32, BF, I32, U16, Q4, U8 = "float32", "bfloat16", "int32", "uint16", "float8_e4m3fn_x4", "uint8"
+
+SCRATCH = {}
+for _n, _w, _d in [
+    ("X", 4 * C, BF), ("XH", 4 * C2, BF), ("E", 4 * C2, BF), ("ut", 512, BF), ("vt", 512, BF), ("Z", 4 * PW, BF), ("U", 8 * UW, BF), ("H", 4 * PW, BF),
+    ("Lt", 512, BF), ("eb", 2048, BF), ("ones", 512, BF), ("zeros", M, BF), ("alt", C2, BF),
+    ("qx", C, Q4), ("sx", C, U8), ("qu", 128, Q4), ("su", 128, U8), ("qur", 128, Q4), ("sur", 128, U8), ("qv", 128, Q4), ("sv", 128, U8),
+    ("qw", 512, Q4), ("sw", 512, U8), ("qe", 512, Q4), ("se", 512, U8), ("qz", PW, Q4), ("sz", PW, U8),
+    ("iot", C, F32), ("iott", 2 * C, F32), ("K", C, F32), ("Kb", C, BF), ("j16", 16, F32), ("k16", 64, F32), ("qo", 28, U16), ("iW", 28, F32),
+    ("dm", M, F32), ("keep", M, F32), ("m01", 32, F32), ("mbig", 32, F32), ("j2", 32, F32),
+    ("pi", 8, I32), ("pf", 4, F32), ("fx", 16, F32), ("ui", 8, I32), ("uo", 8, U16), ("twi", 28, I32), ("tw0", 28, U16),
+    ("S", C, F32), ("S2", C, F32), ("d", C2, F32), ("thr0", C2, F32), ("thr1", C2, F32), ("un", C, BF), ("c2", C, BF), ("key", C, BF), ("kt", C, BF),
+    ("cvb", C, BF), ("cvk", C, BF), ("cvt", C, BF), ("w1", 28, F32), ("w2", 28, F32), ("w3", 28, F32),
+    ("destW", 28, U16), ("kW", 28, U16), ("cW", 28, U16), ("R1", 2 * PW, F32), ("cvo", PW, F32), ("cvq", PW, F32),
+    ("oW", 16, U16), ("vW", 16, U16), ("bR", PW, BF), ("cvz", PW, BF), ("bW", 16, U16),
+    ("dU", M, F32), ("dM", M, F32), ("dS", M, F32), ("junk", 26 * M, BF), ("Mw", 48, F32), ("lb", 16, F32), ("xB", 32, F32),
+    ("r3", 4, F32), ("T3", 96, F32), ("T4", 96, F32), ("r4", 4, F32), ("tau", 4, F32),
+    ("eq", M, BF), ("cum", M, BF), ("sg", M, BF), ("e1", M, BF), ("LV", PW, F32), ("sig", C, BF), ("cg", C, BF), ("u2", C, BF),
+    ("a0", C, F32), ("cvp", C, F32), ("p1", 28, F32), ("p2", 28, F32), ("p3", 28, F32), ("posW", 28, U16), ("R2", C, F32), ("cvr", C, F32), ("pW", 28, U16),
+    ("pt", C2, F32), ("pu", C2, F32), ("ptp", C, F32), ("cvn", C, F32), ("twS", 20, U16), ("yo", C, F32), ("oto", C, F32),
+]:
+    SCRATCH[_n] = ("sbuf", [128, _w], _d)
+for _t in range(R):
+    for _n, _w, _d in [("ql", 128, Q4), ("sl", 128, U8), ("nl", 8, U16), ("lq", 128, Q4), ("ls", 128, U8), ("ln", 8, U16)]:
+        SCRATCH["%s%d" % (_n, _t)] = ("sbuf", [128, _w], _d)
+SCRATCH["ps"] = ("psum", [128, 512 * 8], F32)
+
+SEMAPHORES = ["cV", "cA", "cT", "cG", "sent"] + ["arrL%d" % t for t in range(R)] + ["arrC%d" % t for t in range(R)] + ["dm%d" % k for k in range(24)]
+
+ORDER = {
+    "V": "15 0 11 1 3 2 5 13 4 10 9 8 21 12 6-7 28 17 23 27 24-26 30-31 29 32-35 108 19 36 38-42 44 46 43 45 16 37 51-52 48 50 53 49 14 22 47 54 107 56 20 58 55 59 57 61 60 18 62 65-76 64 77-80 63 84 81 86 82-83 85 91 87-90 92-98 101-103 99-100 104 106 105 109-118 120-121 123 119 133 122 129 134-137 124 130 138-144 127 145 157 126 147 131 125 146 152 148 128 132 153 150 154 151 149 155-156 158-159 163 160 162 161 164 167-168 170 169 172 171 174 173 175-179 166 180-183 165 184-186 189 188 190 194 191-193 187 195-197 199 198 200-201 205 204 206 202-203 207 209 208 210-214 216-219 221-222 224 220 234 223 230-231 225 235-239 226 241 229 242-246 248 227 232 228 247 215 233 240 250 249 252 258 251 253 256 254 257 255 261-262 264 263 265 268-269 259 271 270 273 272 275 274 276 260 277-280 266 281-284 267 288 285-287 289 291-294 296-297 295 299-300 302 298 301 290 305 303-304 306-309 311 310",
+    "A": "0-1 22 4 3 30 10 6 19 12 20 8 13 16 11 15 21 2 18 5 7 17 24 26 9 14 27 25 28 23 29 32 34 31 36 35 33 49 46 48 52 51 50 47 38 37 40-42 44 43 39 45 57 55 53 58 56 61 54 59 62-63 60 64 68 67 65-66 69-80 83-84 81-82 87 85-86 90 92 91 103 94 88 101 98 93 89 99-100 109 104 107-108 106 117 105 97 124-125 114 121 96 110 102 111-113 95 123 120 119 115 118 122 116 130 128 126 131 129 138 134 127 139 135-137 140 132 142 133 144-146 143 141 147-149 151 150 152-157 159 158 162 160 165 161 164 174 167 170 178 175 171 173 166 163 176 172 169 183 181-182 184 179-180 186 200 199 168 188 185 192 191 194 198 196 189 187 193 197 190 177 195 205-206 201-202 207 203 209 208 204 210-212 216 213 215 214 218 217 219 224 222-223 225-226 221 220 227 229-232 228 235 233-234 236",
+    "T": "2-3 0-1 4-5 7 6 8-9 12-13 10-11 14-22 24 23 25-26 28 27 29-35",
+    "G": "0 3 2 4 1 11 7 10 8 5 9 12 6 13-15 18 16 19 17 22-23 21 20 24-26 28-29 27 30 33-34 32 31 35-37",
+    "Y": "0-4 6 5 7 9 8",
+}
+
+
+def rank_program(g, core, T, topo):
+    rank = T.rank_of(core)
+    if rank is None:
+        return
+    n_ranks = len(T.cores)
+    queue = {"V": g.vector, "A": g.scalar, "T": g.tensor, "G": g, "Y": g.sync}
+    ops = []
+    seen = {}
+    n_dma = [0]
+
+    def ap(v):
+        return T[v[0]][:, v[1]:v[2]:v[3]] if v[3] != 1 else T[v[0]][:, v[1]:v[2]]
+
+    def B(name, lo=0, hi=None, step=1):
+        return (name, lo, SCRATCH[name][1][1] if hi is None else hi, step)
+
+    def col(name, c):
+        return (name, c, c + 1, 1)
+
+    def add(q, emit, reads, writes, stream=None, arrivals=()):
+        acc = []
+        for vs, w in ((reads, False), (writes, True)):
+            for v in vs:
+                if v[0] == "ps":
+                    acc.append(("ps", v[1] // 512 * 512, v[1] // 512 * 512 + 512, 1, True))
+                else:
+                    acc.append((v[0], v[1], v[2], v[3], w))
+        deps = set()
+        for n, lo, hi, st, w in acc:
+            for l2, h2, s2, w2, k in seen.get(n, ()):
+                if lo < h2 and l2 < hi and (w or w2) and not (st == s2 and (lo - l2) % st):
+                    deps.add(k)
+        ops.append((q, emit, deps, stream or "c" + q, arrivals))
+        for n, lo, hi, st, w in acc:
+            lst = seen.setdefault(n, [])
+            if w:
+                lst[:] = [e for e in lst if not (lo <= e[0] and e[1] <= hi and (st == 1 or (st == e[2] and (lo - e[0]) % st == 0)))]
+            lst.append((lo, hi, st, w, len(ops) - 1))
+
+    def src(v):
+        if len(v) == 2:
+            return ap(v[0]).indirect(ap(v[1])), [v[0], v[1]]
+        return ap(v), [v]
+
+    def sc(s):
+        return (ap(s), [s]) if isinstance(s, tuple) else (s, [])
+
+    def ts(out, in0, s1, op0, s2=None, op1=None):
+        a, r = src(in0)
+        b, r1 = sc(s1)
+        c, r2 = sc(s2)
+        if op1 is None:
+            add("V", lambda: g.vector.tensor_scalar(ap(out), a, b, None, op0), r + r1, [out])
+        else:
+            add("V", lambda: g.vector.tensor_scalar(ap(out), a, b, c, op0, op1), r + r1 + r2, [out])
+
+    def tt(out, in0, in1, op, arr=()):
+        a, r = src(in0)
+        add("V", lambda: g.vector.tensor_tensor(ap(out), a, ap(in1), op), r + [in1], [out], arrivals=arr)
+
+    def cp(out, in_, arr=()):
+        a, r = src(in_)
+        add("V", lambda: g.vector.tensor_copy(ap(out), a), r, [out], arrivals=arr)
+
+    def scatter(win, off, in_):
+        add("V", lambda: g.vector.tensor_copy(ap(win).indirect(ap(off)), ap(in_)), [off, in_], [win])
+
+    def scan(out, d0, d1, init, op0, op1):
+        b, r = sc(init)
+        add("V", lambda: g.vector.tensor_tensor_scan(ap(out), ap(d0), ap(d1), b, op0, op1), [d0, d1] + r, [out])
+
+    def red(out, in_, op):
+        add("V", lambda: g.vector.tensor_reduce(ap(out), ap(in_), AX.X, op), [in_], [out])
+
+    def fill(out, c):
+        add("V", lambda: g.vector.memset(ap(out), c), [], [out])
+
+    def act(out, in_, func, bias=None, scale=None, accum=None, arr=()):
+        a, r = src(in_)
+        kw = {}
+        for k, s in (("bias", bias), ("scale", scale)):
+            if s is not None:
+                kw[k], r1 = sc(s)
+                r = r + r1
+        if accum is not None:
+            kw["accum_out"] = ap(accum)
+        add("A", lambda: g.scalar.activation(ap(out), a, func, **kw), r, [out] + ([accum] if accum else []), arrivals=arr)
+
+    def pool_copy(out, in_, n):
+        add("G", lambda: g.affine_select(ap(out), ap(in_), [[0, n]], ALU.is_equal, 0.0, 0, 0), [in_], [out])
+
+    def quant(qn, sn, lo, hi, tile, t0):
+        t = B(tile, 4 * t0, 4 * (t0 + hi - lo))
+        add("V", lambda: g.vector.quantize_mx(ap(B(qn, lo, hi)), ap(B(sn, lo, hi)), ap(t)), [t], [B(qn, lo, hi), B(sn, lo, hi)])
+
+    def bank(k, n):
+        return B("ps", 512 * k, 512 * k + n)
+
+    def mm(k, n, wq, ws, w0, xq, xs, x0, arr=()):
+        o = bank(k, n)
+        r = [B(wq, w0, w0 + 128), B(ws, w0, w0 + 128), B(xq, x0, x0 + n), B(xs, x0, x0 + n)]
+        add("T", lambda: g.tensor.matmul_mx(ap(o), ap(r[0]), ap(r[1]), ap(r[2]), ap(r[3]), True, True), r, [o], arrivals=arr)
+
+    def dma(q, out, in_, reads, writes):
+        s = "dm%d" % n_dma[0]
+        n_dma[0] += 1
+        add(q, lambda: queue[q].dma_start(out, in_), reads, writes, stream=s)
+
+    def iota(out, pattern, base, cm):
+        if SCRATCH[out[0]][2] == I32:
+            add("G", lambda: g.iota(ap(out), pattern, base, cm), [], [out])
+        else:
+            add("G", lambda: g.iota(ap(out), pattern, base, cm, allow_small_or_imprecise_dtypes=True), [], [out])
+
+    def conv(out, in_, n, k="K"):
+        scan(out, B(k, 0, n), in_, 0.0, ALU.add, ALU.min)
+
+    def wr(name, lo, hi):
+        return B(name, lo + 15, hi, 16)
+
+    def pair(name, half, lo=0, hi=C, plane=0):
+        return B(name, C2 * plane + 2 * lo + half, C2 * plane + 2 * hi, 2)
+
+    def plane(name, p):
+        return B(name, C2 * p, C2 * p + C2)
+
+    fixes = [(BIG, 0.0), (-512.0, 1.0), (1024.0, 0.0), (512.0, 0.0), (256.0, 0.0), (BIG / 2, -1.0), (-BIG, 0.0), (2 * BIG, 0.0), (2 * BIG, 1.0)]
+    FI, FM, F2, F1, FC, FP, FN, FE, FO = [col("fx", k) for k in range(9)]
+
+    dma("Y", ap(B("X", 0, 4 * ST)), T.x[:, 0:4 * ST], [], [B("X", 0, 4 * ST)])
+    dma("A", ap(B("ut")), T.u[:, :], [], [B("ut")])
+    dma("A", ap(B("X", 4 * ST, 4 * C)), T.x[:, 4 * ST:4 * C], [], [B("X", 4 * ST, 4 * C)])
+    dma("Y", ap(B("twi")), T.tw[:, :], [], [B("twi")])
+    dma("Y", ap(B("qw")).bitcast(dt.uint8), T.wc[:, :], [], [B("qw")])
+    dma("Y", ap(B("sw")), T.ws[:, :], [], [B("sw")])
+    dma("Y", ap(B("vt")), T.v[:, :], [], [B("vt")])
+
+    iota(B("pi", 0, 4), [[1, 2], [0, 2]], 0, 1)
+    iota(B("j16"), [[1, 16]], 0, 0)
+    iota(B("ui"), [[16, 8]], 0, 0)
+    iota(B("iot"), [[1, C]], 0, 0)
+    iota(B("j2"), [[1, 2], [0, 16]], 0, 0)
+    fill(B("zeros"), 0.0)
+    ts(B("pi", 5, 7), B("pi", 1, 3), 15, ALU.bitwise_and)
+    ts(B("pi", 4, 5), B("pi", 0, 1), 4, ALU.logical_shift_right, 1, ALU.bitwise_and)
+    fill(B("ones"), 1.0)
+    cp(B("pf", 0, 3), B("pi", 4, 7))
+    fill(B("R1"), 0.0)
+    ts(col("pf", 3), col("pf", 1), 15.0, ALU.not_equal)
+    ts(B("qo"), B("zeros", 0, 28), col("pf", 1), ALU.add)
+    ts(B("k16", 16, 32), B("j16"), col("pf", 1), ALU.is_equal, 2 * BIG, ALU.mult)
+    ts(B("k16", 32, 48), B("j16"), col("pf", 2), ALU.is_equal, -BIG, ALU.mult)
+    ts(B("k16", 48, 64), B("j16"), 0.0, ALU.not_equal)
+    fill(B("U", 0, 4 * UW), 0.0)
+    tt(B("k16", 0, 16), B("k16", 16, 32), B("k16", 32, 48), ALU.add)
+    cp(B("uo"), B("ui"))
+    fill(B("LV"), 0.0)
+    fill(B("Mw", 16, 32), 0.0)
+    fill(B("H"), 0.0)
+    fill(pair("alt", 0), 0.0)
+    fill(pair("alt", 1), 1.0)
+    ts(B("m01"), B("j2"), col("pf", 0), ALU.is_equal)
+    ts(B("mbig"), B("j2"), col("pf", 0), ALU.not_equal, 1024 * HUGE, ALU.mult)
+    ts(B("p1"), B("iot", 0, C, 16), col("pf", 1), ALU.add)
+    ts(B("iW"), B("p1"), 2.0, ALU.mult, 2.0 * (LV2 + 1), ALU.add)
+    act(B("K"), (B("k16", 0, 16), B("qo")), AF.Copy)
+    act(B("iott", 0, C), B("iot"), AF.Copy, scale=TINY)
+    act(B("iott", C, 2 * C), B("iot"), AF.Copy, scale=TINY)
+    act(B("Kb"), B("K"), AF.Copy, scale=512.0 / BIG)
+    for k, (a, b) in enumerate(fixes):
+        act(col("fx", k), col("pf", 3), AF.Identity, bias=b, scale=a)
+
+    quant("qu", "su", 0, 128, "ut", 0)
+    add("V", lambda: g.vector.tensor_copy(ap(B("qur")).bitcast(dt.uint32), ap(B("qu")).bitcast(dt.uint32).indirect(ap(B("uo")))), [B("qu"), B("uo")], [B("qur")])
+    add("V", lambda: g.vector.tensor_copy(ap(B("sur")), ap(B("su")).indirect(ap(B("uo")))), [B("su"), B("uo")], [B("sur")])
+
+    def scores(lo, hi, banks):
+        quant("qx", "sx", lo, hi, "X", lo)
+        for k in banks:
+            mm(k, hi - lo, "qur", "sur", 0, "qx", "sx", lo)
+        if banks:
+            act(B("S", lo, hi), bank(banks[-1], hi - lo), AF.Copy)
+
+    def planes(lo, hi):
+        for p in range(4):
+            pool_copy(pair("XH", 0, lo, hi, p), B("X", 4 * lo + p, 4 * hi, 4), hi - lo)
+
+    def ties(thr, lo, hi, tw, arr=()):
+        tt(pair(thr, 1, lo, hi), (B("iott", lo, hi), tw), B("iott", C + lo, C + hi), ALU.subtract, arr=arr)
+
+    def under_a(thr, lo, hi, tw):
+        n, a, b = hi - lo, lo // 16, hi // 16
+        d = pair("d", 0, lo, hi)
+        if lo:
+            tt(d, B("S2", lo, hi), bank(1, n), ALU.subtract)
+        else:
+            tt(d, (B("S", lo, hi), tw), B("S2", lo, hi), ALU.subtract)
+        tt(B("un", lo, hi), d, pair(thr, 1, lo, hi), ALU.is_gt)
+        scan(B("c2", lo, hi), B("un", lo, hi), B("un", lo, hi), col("c2", lo - 1) if lo else 2.0, ALU.add, ALU.add)
+        scan(B("key", lo, hi), B("c2", lo, hi), B("un", lo, hi), 0.0, ALU.max, ALU.mult)
+        act(B("kt", lo, hi), (B("key", lo, hi), tw), AF.Copy)
+        conv(B("cvk", lo, hi), B("key", lo, hi), n, "Kb")
+        conv(B("cvb", lo, hi), B("c2", lo, hi), n, "Kb")
+        ts(B("w1", a, b), wr("cvk", lo, hi), FM, ALU.max)
+        conv(B("cvt", lo, hi), B("kt", lo, hi), n, "Kb")
+        tt(B("w2", a, b), wr("cvt", lo, hi), B("w1", a, b), ALU.add)
+        ts(B("destW", a, b), B("w2", a, b), F2, ALU.add)
+
+    def under_b(lo, hi):
+        scatter(B("R1"), B("destW", lo // 16, hi // 16), B("iot", lo, hi))
+
+    def rank_part(k0, k1):
+        a, b, n = k0 // 16, k1 // 16, k1 - k0
+        top = C if k1 == M else ST
+        conv(B("cvo", k0, k1), B("R1", 4 + 2 * k0, 4 + 2 * k1, 2), n)
+        conv(B("cvq", k0, k1), B("R1", 5 + 2 * k0, 4 + 2 * k1, 2), n)
+        ts(B("oW", a, b), wr("cvo", k0, k1), 2.0, ALU.mult, FE, ALU.add)
+        ts(B("vW", a, b), wr("cvq", k0, k1), FI, ALU.add)
+        act(B("dU", k0, k1), (B("d", 0, 2 * top), B("oW", a, b)), AF.Copy)
+        act(B("bR", k0, k1), (B("c2", 0, top), B("vW", a, b)), AF.Copy)
+        for p in range(4):
+            u1 = B("U", UW * p + 2 + k0, UW * p + 2 + k1)
+            act(u1, (B("XH", C2 * p, C2 * p + 2 * top), B("oW", a, b)), AF.Copy, scale=0.5)
+            cp(B("U", UW * (4 + p) + 2 + k0, UW * (4 + p) + 2 + k1), u1)
+        scan(B("dM", k0, k1), B("dU", k0, k1), B("dm", k0, k1), 0.0, ALU.max, ALU.min)
+        scan(B("dS", k0, k1), B("keep", k0, k1), B("dM", k0, k1), 0.0, ALU.mult, ALU.add)
+        conv(B("cvz", k0, k1), B("bR", k0, k1), n, "Kb")
+        ts(B("bW", a, b), wr("cvz", k0, k1), 0.5, ALU.mult, FC, ALU.add)
+        for c in range(b):
+            lo, j = (k0, 16) if c < a else (0, 0)
+            o = M * (c + j)
+            act(B("junk", o + lo, o + k1), B("dU", lo, k1), AF.Sign, bias=col("dS", 16 * c + 15), scale=-1.0, accum=col("Mw", c + j))
+
+    def e_plane(p):
+        h = (B("H", PW * p, PW * p + PW), B("cW"))
+        if p in BY_SCAN:
+            act(pair("XH", 1, 0, C, p), h, AF.Copy)
+            scan(plane("E", p), B("alt"), plane("XH", p), 0.0, ALU.mult, ALU.add)
+        else:
+            tt(pair("E", 1, 0, C, p), h, B("X", p, 4 * C, 4), ALU.add)
+
+    def h_plane(b):
+        act(col("H", PW * b + 1), B("ps", 512 * (2 + b) + M - 1, 512 * (2 + b) + M), AF.Copy, scale=0.03125)
+        act(B("H", PW * b + 2, PW * b + M + 2), bank(2 + b, M), AF.Copy, scale=0.03125)
+
+    def middle(t, pieces):
+        rank_part(ST // 2 if t else 0, M)
+        du = B("dU")
+        act(B("U", 1, 4 * UW, UW), B("U", M + 1, 4 * UW, UW), AF.Copy)
+        act(B("U", 4 * UW + 1, 8 * UW, UW), B("U", M + 1, 4 * UW, UW), AF.Copy)
+        tt(B("w3"), wr("cvt", 0, C), wr("cvk", 0, C), ALU.add)
+        ts(B("cW"), wr("cvb", 0, C), 0.5, ALU.mult, FC, ALU.add)
+        ts(B("kW"), B("w3"), 0.5, ALU.mult, F1, ALU.add)
+        for p in range(4):
+            a2 = UW * (4 + p)
+            tt(B("Z", p, 4 * M, 4), (B("U", UW * p, UW * p + PW), B("bW", 0, 14)), B("U", a2 + 1, a2 + 1 + M), ALU.add)
+        quant("qz", "sz", 0, M, "Z", 0)
+        for b in range(4):
+            mm(2 + b, M, "qw", "sw", 128 * b, "qz", "sz", 0)
+        h_plane(0)
+        h_plane(1)
+        e_plane(0)
+        e_plane(1)
+        if t:
+            tt(B("Mw", 32, 46), B("Mw", 0, 14), B("Mw", 16, 30), ALU.add)
+        mw, dw, xb, xa = B("Mw", 32, 46) if t else B("Mw", 0, 14), wr("dS", 0, M), B("xB", 0, 14), B("xB", 16, 30)
+        act(B("junk", 14 * M, 14 * M + 14), mw, AF.Sign, bias=-96.5, scale=-1.0, accum=col("r3", 2))
+        ts(B("lb", 0, 14), mw, -96.5, ALU.is_le, HUGE, ALU.mult)
+        act(B("T3", 64, 96), B("m01"), AF.Identity, scale=col("r3", 2))
+        h_plane(2)
+        tt(xb, dw, B("lb", 0, 14), ALU.add)
+        tt(xa, dw, B("lb", 0, 14), ALU.min)
+        red(col("r3", 0), xb, ALU.min)
+        red(col("r3", 1), xa, ALU.max)
+        ts(B("T3", 0, 32), B("mbig"), col("r3", 0), ALU.add)
+        ts(B("T3", 32, 64), B("m01"), col("r3", 1), ALU.mult)
+        add("V", lambda: g.vector.transpose(ap(B("T4")), ap(B("T3"))), [B("T3")], [B("T4")])
+        act(B("T3", 64, 96), B("T4", 64, 96), AF.Identity, accum=col("r4", 2))
+        red(col("r4", 0), B("T4", 0, 32), ALU.min)
+        red(col("r4", 1), B("T4", 32, 64), ALU.max)
+        ts(col("tau", 0), col("r4", 2), -97.0, ALU.is_lt, col("r4", 0), ALU.mult)
+        ts(col("tau", 1), col("tau", 0), col("r4", 1), ALU.max)
+        tau = col("tau", 1)
+        act(B("sg"), du, AF.Sign, bias=tau, scale=-1.0)
+        ts(B("eq"), du, tau, ALU.is_equal, 1.0 / 256, ALU.mult)
+        act(B("junk", 15 * M, 16 * M), B("sg"), AF.Relu, accum=col("tau", 2))
+        act(B("e1"), B("sg"), AF.Identity, bias=1.0)
+        h_plane(3)
+        ts(col("tau", 3), col("tau", 2), -1.0 / 256, ALU.mult, 64.5 / 256, ALU.add)
+        scan(B("cum"), B("zeros"), B("eq"), col("tau", 3), ALU.add, ALU.subtract)
+        scan(B("LV", 2, 2 + M), B("cum"), B("e1"), 4.0, ALU.min, ALU.add)
+        act(B("sig"), (B("LV"), B("kW")), AF.Sign, bias=-1.0)
+        scan(B("cg"), B("sig"), B("ones", 0, C), 0.0, ALU.add, ALU.add)
+        scan(B("u2"), B("cg"), B("sig"), 0.0, ALU.max, ALU.mult)
+        conv(B("cvp"), B("u2"), C)
+        e_plane(2)
+        ts(B("p1"), wr("cvp", 0, C), FN, ALU.is_le)
+        scan(B("a0"), B("ones", 0, C), B("sig"), 0.0, ALU.add, ALU.subtract)
+        tt(B("p2"), B("p1"), B("iW"), ALU.mult)
+        tt(B("p3"), B("p2"), wr("cvp", 0, C), ALU.add)
+        ts(B("posW"), B("p3"), 0.5, ALU.mult, FP, ALU.add)
+        scatter(B("R2"), B("posW"), B("iot"))
+        e_plane(3)
+        for lo, hi, tw in pieces:
+            act(pair("pt", 1, lo, hi), (B("cg", lo, hi), tw), AF.Copy)
+        for lo, hi, tw in pieces:
+            act(pair("pu", 1, lo, hi), (B("a0", lo, hi), tw), AF.Copy)
+        conv(B("cvr", 0, LV2), B("R2", 0, LV2), LV2)
+
+    def remote(out, in_, reads, sem, dst, mask):
+        rid, pid, _ = topo.addr(dst)
+        add("G", lambda: g.remote_dma(out, in_, T.sem[sem], T.sem.sent, pid, rid, mask), reads, [], stream="remote")
+
+    sent = [0]
+
+    def send(t):
+        dst = T.cores[(rank + STEP[t]) % n_ranks]
+        eng = topo.engines(core, dst)
+        half = len(eng) // 2
+        masks = [sum(1 << e for e in es) for es in (eng, eng[:half], eng[half:])]
+        ls = B("pW", 0, 8)
+        ts(ls, wr("cvr", 0, LV2), 2.0, ALU.mult, FO, ALU.add)
+        conv(B("cvr", LV2, C), B("R2", LV2, C), ST)
+        for p in range(2):
+            act(B("Lt", p, 512, 4), (plane("E", p), ls), AF.Copy)
+            cp(B("Lt", 2 + p, 512, 4), (plane("E", 2 + p), ls))
+        act(B("ptp", 0, LV2), (B("pt"), ls), AF.Copy)
+        ts(B("pW", 8, 28), wr("cvr", LV2, C), 2.0, ALU.mult, FO, ALU.add)
+        quant("ql%d" % t, "sl%d" % t, 0, 128, "Lt", 0)
+        remote(ap(B("lq%d" % t)).bitcast(dt.uint8), ap(B("ql%d" % t)).bitcast(dt.uint8), [B("ql%d" % t)], "arrC%d" % t, dst, masks[1])
+        remote(ap(B("ls%d" % t)), ap(B("sl%d" % t)), [B("sl%d" % t)], "arrC%d" % t, dst, masks[2])
+        conv(B("cvn", 0, LV2), B("ptp", 0, LV2), LV2)
+        ts(B("nl%d" % t), wr("cvn", 0, LV2), 0.5, ALU.mult, FP, ALU.add)
+        remote(ap(B("ln%d" % t)), ap(B("nl%d" % t)), [B("nl%d" % t)], "arrL%d" % t, dst, masks[0])
+        sent[0] += len(eng) + 2 * half
+        back = topo.engines(T.cores[(rank - STEP[t]) % n_ranks], core)
+        return [("arrL%d" % t, len(back))], [("arrC%d" % t, len(back) // 2 * 2)]
+
+    def stay(thr_old, thr_new):
+        qs = B("pW", 8, 28)
+        for p in range(2):
+            act(B("X", p, 4 * ST, 4), (plane("E", p), qs), AF.Copy)
+            cp(B("X", 2 + p, 4 * ST, 4), (plane("E", 2 + p), qs))
+        act(B("ptp", LV2, C), (B("pu"), qs), AF.Copy)
+        scores(0, ST, (6, 0) if thr_new else ())
+        if thr_new:
+            planes(0, ST)
+            conv(B("cvn", LV2, C), B("ptp", LV2, C), ST)
+            ts(B("twS"), wr("cvn", LV2, C), 0.5, ALU.mult, FP, ALU.add)
+            cp(B("S2", 0, ST), bank(6, ST))
+            act(pair(thr_new, 1, 0, ST), (B(thr_old), qs), AF.Copy)
+
+    def unpack(t, arr_c):
+        for b in range(4):
+            mm(2 + b, 128, "qe", "se", 128 * b, "lq%d" % t, "ls%d" % t, 0, arr=arr_c)
+        for b in range(4):
+            act(B("X", 4 * ST + b, 4 * C, 4), bank(2 + b, 128), AF.Copy)
+
+    scores(0, ST, (0, 6))
+    scores(ST, C, (1, 7))
+    planes(0, C)
+    cp(B("tw0"), B("twi"))
+    cp(B("S2", 0, ST), bank(0, ST))
+    cp(B("S2", ST, C), bank(1, LV2))
+    ties("thr0", 0, C, B("tw0"))
+    act(B("dm"), (B("k16", 16, 32), B("qo", 0, 14)), AF.Copy, scale=HUGE / (2 * BIG))
+    act(B("keep"), (B("k16", 48, 64), B("qo", 0, 14)), AF.Copy)
+    for p in range(4):
+        act(pair("XH", 1, 0, C, p), B("iot"), AF.Copy)
+    act(pair("d", 1), B("iot"), AF.Copy)
+    under_a("thr0", 0, C, B("tw0"))
+    for name, half in (("thr0", 0), ("thr1", 0), ("pt", 0), ("pu", 0)):
+        act(pair(name, half), B("iot"), AF.Copy)
+    for p in range(4):
+        if p not in BY_SCAN:
+            act(pair("E", 0, 0, C, p), B("iot"), AF.Copy)
+    under_b(0, C)
+    for b in range(4):
+        o = B("eb", 512 * b, 512 * b + 512)
+        add("G", lambda o=o, b=b: g.affine_select(ap(o), ap(B("ones")), [[-1, 512]], ALU.is_equal, 0.0, b, 4), [B("ones")], [o])
+    pieces = [(0, C, B("tw0"))]
+    for t in range(R):
+        middle(t, pieces)
+        arr_l, arr_c = send(t)
+        last = t == R - 1
+        old, new = "thr%d" % (t % 2), "thr%d" % (1 - t % 2)
+        stay(old, None if last else new)
+        if t == 0:
+            quant("qe", "se", 0, 512, "eb", 0)
+            quant("qv", "sv", 0, 128, "vt", 0)
+        twa = B("ln%d" % t)
+        if last:
+            break
+        under_a(new, 0, ST, B("twS"))
+        unpack(t, arr_c)
+        scores(ST, C, (1,))
+        planes(ST, C)
+        act(B("S2", ST, C), (B("S", ST, C), twa), AF.Copy, arr=arr_l)
+        under_b(0, ST)
+        rank_part(0, ST // 2)
+        ties(new, ST, C, twa, arr=arr_l)
+        under_a(new, ST, C, twa)
+        under_b(ST, C)
+        pieces = [(0, ST, B("twS")), (ST, C, twa)]
+
+    def finish(lo, hi, k):
+        mm(k, hi - lo, "qv", "sv", 0, "qx", "sx", lo)
+        dma("Y", T.oc[:, 4 * lo:4 * hi], ap(B("qx", lo, hi)).bitcast(dt.uint8), [B("qx", lo, hi)], [])
+        cp(B("yo", lo, hi), bank(k, hi - lo))
+        dma("Y", T.y[:, lo:hi], ap(B("yo", lo, hi)), [B("yo", lo, hi)], [])
+
+    finish(0, ST, 0)
+    act(B("oto", 0, ST), B("ptp", LV2, C), AF.Identity, bias=-1.0, scale=0.5)
+    unpack(R - 1, arr_c)
+    scores(ST, C, ())
+    finish(ST, C, 1)
+    for k in range(4):
+        dma("A", T.osc[4 * k:4 * k + 4, :], T.sx[32 * k:32 * k + 4, :], [B("sx")], [])
+    cp(B("oto", ST, C), (B("iot", ST, C), twa), arr=arr_l)
+    dma("Y", T.ot[:, :], T.oto[0:128:16, :], [B("oto")], [])
+
+    order = list(range(len(ops)))
+    if ORDER:
+        line = {}
+        for q in queue:
+            mine = [k for k in order if ops[k][0] == q]
+            runs = [[int(x) for x in w.split("-")] for w in ORDER[q].split()]
+            line[q] = [mine[i] for r in runs for i in range(r[0], r[-1] + 1)][::-1]
+            assert sorted(line[q]) == mine
+        order, done = [], set()
+        while len(order) < len(ops):
+            k = [line[q].pop() for q in queue if line[q] and ops[line[q][-1]][2] <= done][:]
+            assert k
+            order += k
+            done |= set(k)
+    known = {q: {} for q in queue}
+    clock, token, place, waits, needed = {}, {}, {}, {}, set()
+    for k in order:
+        q, emit, deps, stream, arrivals = ops[k]
+        mine = known[q]
+        waits[k] = []
+        for j in sorted(deps, key=lambda j: -token[j][1]):
+            s, p = token[j]
+            if mine.get(s, 0) < p:
+                waits[k].append(j)
+                needed.add(j)
+                mine[s] = p
+                for s2, p2 in clock[j].items():
+                    mine[s2] = max(mine.get(s2, 0), p2)
+        for s, n in arrivals:
+            if s not in mine:
+                mine[s] = 1
+                waits[k].append((s, n))
+        place[stream] = place.get(stream, 0) + 1
+        token[k] = (stream, place[stream])
+        clock[k] = dict(mine)
+    count, value = {}, {}
+    for k in order:
+        q, (s, p) = ops[k][0], token[k]
+        for w in waits[k]:
+            if isinstance(w, tuple):
+                queue[q].wait_ge(T.sem[w[0]], w[1])
+            else:
+                queue[q].wait_ge(T.sem[token[w][0]], value[w])
+        ins = ops[k][1]()
+        if s != "remote" and (k in needed or p == place[s]):
+            n = 16 if s.startswith("dm") else 1
+            ins.then_inc(T.sem[s], n)
+            count[s] = count.get(s, 0) + n
+            value[k] = count[s]
+    for s, n in count.items():
+        g.wait_ge(T.sem[s], n)
+    g.wait_ge(T.sem.sent, sent[0])

@@ -20,14 +20,14 @@ for _n, _w, _d in [
     ("iot", C, F32), ("iott", 2 * C, F32), ("K", C, F32), ("Kb", C, BF), ("j16", 16, F32), ("k16", 64, F32), ("qo", 28, U16), ("iW", 28, F32),
     ("dm", M, F32), ("keep", M, F32), ("m01", 32, F32), ("mbig", 32, F32), ("j2", 32, F32),
     ("pi", 8, I32), ("pf", 4, F32), ("fx", 16, F32), ("ui", 8, I32), ("uo", 8, U16), ("twi", 28, I32), ("tw0", 28, U16),
-    ("S", C, F32), ("S2", C, F32), ("d", C2, F32), ("thr0", C2, F32), ("thr1", C2, F32), ("un", C, BF), ("c2", C, BF), ("key", C, BF), ("kt", C, BF),
+    ("S", C, F32), ("S2", C, F32), ("d", C2, F32), ("thr0", C2, F32), ("thr1", C2, F32), ("un", C, BF), ("c2", C, BF), ("K4", C, BF), ("kt", C, BF),
     ("cvb", C, BF), ("cvk", C, BF), ("cvt", C, BF), ("w1", 28, F32), ("w2", 28, F32), ("w3", 28, F32),
-    ("destW", 28, U16), ("kW", 28, U16), ("cW", 28, U16), ("R1", 2 * PW, F32), ("cvo", PW, F32), ("cvq", PW, F32),
+    ("destW", 28, U16), ("kW", 28, U16), ("cW", 28, U16), ("R1", 512 + 2 * PW, F32), ("cvo", PW, F32), ("cvq", PW, F32),
     ("oW", 16, U16), ("vW", 16, U16), ("bR", PW, BF), ("cvz", PW, BF), ("bW", 16, U16),
     ("dU", M, F32), ("dM", M, F32), ("dS", M, F32), ("junk", 26 * M, BF), ("Mw", 48, F32), ("lb", 16, F32), ("xB", 32, F32),
     ("r3", 4, F32), ("T3", 96, F32), ("T4", 96, F32), ("r4", 4, F32), ("tau", 4, F32),
     ("eq", M, BF), ("cum", M, BF), ("sg", M, BF), ("e1", M, BF), ("LV", PW, F32), ("sig", C, BF), ("cg", C, BF), ("u2", C, BF),
-    ("a0", C, F32), ("cvp", C, F32), ("p1", 28, F32), ("p2", 28, F32), ("p3", 28, F32), ("posW", 28, U16), ("R2", C, F32), ("cvr", C, F32), ("pW", 28, U16),
+    ("a0", C, F32), ("p1", 28, F32), ("p2", 28, F32), ("p3", 28, F32), ("posW", 28, U16), ("R2", C, F32), ("cvr", C, F32), ("pW", 28, U16),
     ("pt", C2, F32), ("pu", C2, F32), ("ptp", C, F32), ("cvn", C, F32), ("twS", 20, U16), ("yo", C, F32), ("oto", C, F32),
 ]:
     SCRATCH[_n] = ("sbuf", [128, _w], _d)
@@ -39,11 +39,11 @@ SCRATCH["ps"] = ("psum", [128, 512 * 8], F32)
 SEMAPHORES = ["cV", "cA", "cT", "cG", "sent"] + ["arrL%d" % t for t in range(R)] + ["arrC%d" % t for t in range(R)] + ["dm%d" % k for k in range(24)]
 
 ORDER = {
-    "V": "15 0 11 1 3 2 5 13 4 10 9 8 21 12 6-7 28 17 23 27 24-26 30-31 29 32-35 108 19 36 38-42 44 46 43 45 16 37 51-52 48 50 53 49 14 22 47 54 107 56 20 58 55 59 57 61 60 18 62 65-76 64 77-80 63 84 81 86 82-83 85 91 87-90 92-98 101-103 99-100 104 106 105 109-118 120-121 123 119 133 122 129 134-137 124 130 138-144 127 145 157 126 147 131 125 146 152 148 128 132 153 150 154 151 149 155-156 158-159 163 160 162 161 164 167-168 170 169 172 171 174 173 175-179 166 180-183 165 184-186 189 188 190 194 191-193 187 195-197 199 198 200-201 205 204 206 202-203 207 209 208 210-214 216-219 221-222 224 220 234 223 230-231 225 235-239 226 241 229 242-246 248 227 232 228 247 215 233 240 250 249 252 258 251 253 256 254 257 255 261-262 264 263 265 268-269 259 271 270 273 272 275 274 276 260 277-280 266 281-284 267 288 285-287 289 291-294 296-297 295 299-300 302 298 301 290 305 303-304 306-309 311 310",
-    "A": "0-1 22 4 3 30 10 6 19 12 20 8 13 16 11 15 21 2 18 5 7 17 24 26 9 14 27 25 28 23 29 32 34 31 36 35 33 49 46 48 52 51 50 47 38 37 40-42 44 43 39 45 57 55 53 58 56 61 54 59 62-63 60 64 68 67 65-66 69-80 83-84 81-82 87 85-86 90 92 91 103 94 88 101 98 93 89 99-100 109 104 107-108 106 117 105 97 124-125 114 121 96 110 102 111-113 95 123 120 119 115 118 122 116 130 128 126 131 129 138 134 127 139 135-137 140 132 142 133 144-146 143 141 147-149 151 150 152-157 159 158 162 160 165 161 164 174 167 170 178 175 171 173 166 163 176 172 169 183 181-182 184 179-180 186 200 199 168 188 185 192 191 194 198 196 189 187 193 197 190 177 195 205-206 201-202 207 203 209 208 204 210-212 216 213 215 214 218 217 219 224 222-223 225-226 221 220 227 229-232 228 235 233-234 236",
-    "T": "2-3 0-1 4-5 7 6 8-9 12-13 10-11 14-22 24 23 25-26 28 27 29-35",
-    "G": "0 3 2 4 1 11 7 10 8 5 9 12 6 13-15 18 16 19 17 22-23 21 20 24-26 28-29 27 30 33-34 32 31 35-37",
-    "Y": "0-4 6 5 7 9 8",
+    "V": "5 11 0-2 10 4 3 17 13 8-9 7 6 12 24 28 26 25 29 27 32 30-31 33-35 21 36-38 16 39-44 22 46 45 23 110 56 20 52 57 47 58 53 51 49 109 48 18 50 54-55 60 14 19 63 62 61 64 67 69 68 71 70 73 72 74 59 75-78 65 79 66 80-81 85 93 83 82 86 84 88 87 89-92 94-96 98 97 99-100 103-105 101 106 108 107 102 111-113 115 114 116-123 136 125 135 124 137 15 138-139 131 141 140 132 126 142-146 129 147 127 148-149 133 130 150 161 134 128 155 152 156 154 153 151 157 159 158 166 165 164 163 160 167 170-171 173 172 175 174 177 176 162 178-182 168 183 169 184-185 189 197 187 186 190 188 192-194 191 195-196 198-204 207-210 212 211 205 213 206 214-227 238 237 228 239 233 240-244 261 245 235 234 246 232 247 263 248-249 251 230 250 231 252 236 256 262 254 229 253 255 259 257 260 258 265-269 272-273 275 274 277 276 279 278 264 280-284 270 285 271 286-287 291 299 289 288 292 290 294-298 300-301 303-304 306 302 305 309 307-308 293 310-315 317 316",
+    "A": "1 0 3 25 4 26 10 2 18 24 6 13 22 21 16-17 5 28 35 14 27 34 30 19 29 15 33 8 32 7 36 31 11 20 23 9 12 37 42 40 39 41 38 45 44 57-58 47 56 48 46 50 54 49 55 52-53 43 51 61 65 63 59 64 71 60 66-67 62 74 68 72 69-70 75 73 77 76 79 78 80-93 95 97 109 98 94 102 100 103 99 105 96 108 110 113 115 114 112 111 123 107 130-131 106 117 104 124 129 120 128 126 125 118 121 127 122 116 101 119 132 136 133 138 137 134 139 144 140 147 141 135 145 143 142 148 146 149 151-154 150 156-158 155 159-161 164 163 162 165-168 173 169 184 170-171 176 181 175 179 182 180 174 172 190 188 187 189 186 185 178 205-206 192 191 183 200 194 197 201 204 193 195 202 198 177 203 196 199 207 211 213 212 208 214 219 215 209 222 210 216 220 217-218 223 221 229 228 225 224 230-232 227 226 233 235-236 234 240 238-239 237",
+    "T": "3 0-2 5-6 4 7-15 18 17 16 19-20 23 22 21 24-26 28-29 27 30 32 31 33-35",
+    "G": "3 1 0 2 4 8 12 10 6 5 11 7 9 13-15 18 22-23 16 19 21 20 17 24-25 29 28 26 30-31 34 27 33 32 35-37",
+    "Y": "0-4 6 5 7-9",
 }
 
 
@@ -173,14 +173,15 @@ def rank_program(g, core, T, topo):
     def plane(name, p):
         return B(name, C2 * p, C2 * p + C2)
 
-    fixes = [(BIG, 0.0), (-512.0, 1.0), (1024.0, 0.0), (512.0, 0.0), (256.0, 0.0), (BIG / 2, -1.0), (-BIG, 0.0), (2 * BIG, 0.0), (2 * BIG, 1.0)]
-    FI, FM, F2, F1, FC, FP, FN, FE, FO = [col("fx", k) for k in range(9)]
+    fixes = [(BIG, 0.0), (-512.0, 1.0), (1024.0, 0.0), (512.0, 0.0), (256.0, 0.0), (BIG / 2, -1.0), (-BIG, 0.0), (2 * BIG, 0.0), (2 * BIG, 1.0),
+             (8192.0, -1537.0), (2044.0, 0.0), (512.0, 1.0), (-9216.0, 2048.0), (256.0, -1.0)]
+    FI, FM, F2, F1, FC, FP, FN, FE, FO, FT, FU, FD, FS, FQ = [col("fx", k) for k in range(14)]
 
     dma("Y", ap(B("X", 0, 4 * ST)), T.x[:, 0:4 * ST], [], [B("X", 0, 4 * ST)])
     dma("A", ap(B("ut")), T.u[:, :], [], [B("ut")])
     dma("A", ap(B("X", 4 * ST, 4 * C)), T.x[:, 4 * ST:4 * C], [], [B("X", 4 * ST, 4 * C)])
     dma("Y", ap(B("twi")), T.tw[:, :], [], [B("twi")])
-    dma("Y", ap(B("qw")).bitcast(dt.uint8), T.wc[:, :], [], [B("qw")])
+    dma("Y", ap(B("qw")).bitcast(dt.uint8), T.wc[:, :], [B("X"), B("ut")], [B("qw")])
     dma("Y", ap(B("sw")), T.ws[:, :], [], [B("sw")])
     dma("Y", ap(B("vt")), T.v[:, :], [], [B("vt")])
 
@@ -211,14 +212,16 @@ def rank_program(g, core, T, topo):
     ts(B("m01"), B("j2"), col("pf", 0), ALU.is_equal)
     ts(B("mbig"), B("j2"), col("pf", 0), ALU.not_equal, 1024 * HUGE, ALU.mult)
     ts(B("p1"), B("iot", 0, C, 16), col("pf", 1), ALU.add)
-    ts(B("iW"), B("p1"), 2.0, ALU.mult, 2.0 * (LV2 + 1), ALU.add)
+    ts(B("p2"), B("p1"), 2.0, ALU.mult, 2.0 * (LV2 + 1), ALU.add)
     act(B("K"), (B("k16", 0, 16), B("qo")), AF.Copy)
     act(B("iott", 0, C), B("iot"), AF.Copy, scale=TINY)
     act(B("iott", C, 2 * C), B("iot"), AF.Copy, scale=TINY)
     act(B("Kb"), B("K"), AF.Copy, scale=512.0 / BIG)
+    act(B("K4"), B("K"), AF.Copy, scale=4.0 / BIG)
     for k, (a, b) in enumerate(fixes):
         act(col("fx", k), col("pf", 3), AF.Identity, bias=b, scale=a)
 
+    ts(B("iW"), B("p2"), F2, ALU.subtract)
     quant("qu", "su", 0, 128, "ut", 0)
     add("V", lambda: g.vector.tensor_copy(ap(B("qur")).bitcast(dt.uint32), ap(B("qu")).bitcast(dt.uint32).indirect(ap(B("uo")))), [B("qu"), B("uo")], [B("qur")])
     add("V", lambda: g.vector.tensor_copy(ap(B("sur")), ap(B("su")).indirect(ap(B("uo")))), [B("su"), B("uo")], [B("sur")])
@@ -246,14 +249,14 @@ def rank_program(g, core, T, topo):
             tt(d, (B("S", lo, hi), tw), B("S2", lo, hi), ALU.subtract)
         tt(B("un", lo, hi), d, pair(thr, 1, lo, hi), ALU.is_gt)
         scan(B("c2", lo, hi), B("un", lo, hi), B("un", lo, hi), col("c2", lo - 1) if lo else 2.0, ALU.add, ALU.add)
-        scan(B("key", lo, hi), B("c2", lo, hi), B("un", lo, hi), 0.0, ALU.max, ALU.mult)
-        act(B("kt", lo, hi), (B("key", lo, hi), tw), AF.Copy)
-        conv(B("cvk", lo, hi), B("key", lo, hi), n, "Kb")
+        act(B("kt", lo, hi), (B("c2", lo, hi), tw), AF.Copy)
+        conv(B("cvk", lo, hi), B("un", lo, hi), n, "K4")
         conv(B("cvb", lo, hi), B("c2", lo, hi), n, "Kb")
-        ts(B("w1", a, b), wr("cvk", lo, hi), FM, ALU.max)
+        ts(B("p3", a, b), wr("cvk", lo, hi), 2048.0, ALU.mult, FT, ALU.add)
+        tt(B("w1", a, b), wr("cvb", lo, hi), B("p3", a, b), ALU.add)
         conv(B("cvt", lo, hi), B("kt", lo, hi), n, "Kb")
-        tt(B("w2", a, b), wr("cvt", lo, hi), B("w1", a, b), ALU.add)
-        ts(B("destW", a, b), B("w2", a, b), F2, ALU.add)
+        tt(B("w2", a, b), wr("cvt", lo, hi), B("w1", a, b), ALU.max)
+        ts(B("destW", a, b), B("w2", a, b), FD, ALU.add)
 
     def under_b(lo, hi):
         scatter(B("R1"), B("destW", lo // 16, hi // 16), B("iot", lo, hi))
@@ -261,7 +264,7 @@ def rank_program(g, core, T, topo):
     def rank_part(k0, k1):
         a, b, n = k0 // 16, k1 // 16, k1 - k0
         top = C if k1 == M else ST
-        conv(B("cvo", k0, k1), B("R1", 4 + 2 * k0, 4 + 2 * k1, 2), n)
+        conv(B("cvo", k0, k1), B("R1", 516 + 2 * k0, 516 + 2 * k1, 2), n)
         conv(B("cvq", k0, k1), B("R1", 5 + 2 * k0, 4 + 2 * k1, 2), n)
         ts(B("oW", a, b), wr("cvo", k0, k1), 2.0, ALU.mult, FE, ALU.add)
         ts(B("vW", a, b), wr("cvq", k0, k1), FI, ALU.add)
@@ -297,9 +300,10 @@ def rank_program(g, core, T, topo):
         du = B("dU")
         act(B("U", 1, 4 * UW, UW), B("U", M + 1, 4 * UW, UW), AF.Copy)
         act(B("U", 4 * UW + 1, 8 * UW, UW), B("U", M + 1, 4 * UW, UW), AF.Copy)
-        tt(B("w3"), wr("cvt", 0, C), wr("cvk", 0, C), ALU.add)
+        ts(B("p2"), wr("cvk", 0, C), 511.0, ALU.mult, FU, ALU.add)
+        tt(B("w3"), B("w2"), B("p2"), ALU.subtract)
         ts(B("cW"), wr("cvb", 0, C), 0.5, ALU.mult, FC, ALU.add)
-        ts(B("kW"), B("w3"), 0.5, ALU.mult, F1, ALU.add)
+        ts(B("kW"), B("w3"), 0.5, ALU.mult, FC, ALU.add)
         for p in range(4):
             a2 = UW * (4 + p)
             tt(B("Z", p, 4 * M, 4), (B("U", UW * p, UW * p + PW), B("bW", 0, 14)), B("U", a2 + 1, a2 + 1 + M), ALU.add)
@@ -332,22 +336,22 @@ def rank_program(g, core, T, topo):
         tau = col("tau", 1)
         act(B("sg"), du, AF.Sign, bias=tau, scale=-1.0)
         ts(B("eq"), du, tau, ALU.is_equal, 1.0 / 256, ALU.mult)
-        act(B("junk", 15 * M, 16 * M), B("sg"), AF.Relu, accum=col("tau", 2))
+        act(B("junk", 15 * M, 16 * M), B("sg"), AF.Relu, scale=1.0 / 256, accum=col("tau", 2))
         act(B("e1"), B("sg"), AF.Identity, bias=1.0)
         h_plane(3)
-        ts(col("tau", 3), col("tau", 2), -1.0 / 256, ALU.mult, 64.5 / 256, ALU.add)
-        scan(B("cum"), B("zeros"), B("eq"), col("tau", 3), ALU.add, ALU.subtract)
-        scan(B("LV", 2, 2 + M), B("cum"), B("e1"), 4.0, ALU.min, ALU.add)
-        act(B("sig"), (B("LV"), B("kW")), AF.Sign, bias=-1.0)
+        scan(B("cum"), B("zeros"), B("eq"), col("tau", 2), ALU.add, ALU.add)
+        scan(B("LV", 2, 2 + M), B("cum"), B("e1"), -4.0, ALU.max, ALU.subtract)
+        act(B("sig"), (B("LV"), B("kW")), AF.Sign, bias=64.5 / 256 - 1, scale=-1.0)
         scan(B("cg"), B("sig"), B("ones", 0, C), 0.0, ALU.add, ALU.add)
-        scan(B("u2"), B("cg"), B("sig"), 0.0, ALU.max, ALU.mult)
-        conv(B("cvp"), B("u2"), C)
+        conv(B("cvb"), B("sig"), C, "K4")
+        conv(B("u2"), B("cg"), C, "Kb")
         e_plane(2)
-        ts(B("p1"), wr("cvp", 0, C), FN, ALU.is_le)
+        ts(B("p1"), wr("cvb", 0, C), -2048.0, ALU.mult, FS, ALU.add)
         scan(B("a0"), B("ones", 0, C), B("sig"), 0.0, ALU.add, ALU.subtract)
-        tt(B("p2"), B("p1"), B("iW"), ALU.mult)
-        tt(B("p3"), B("p2"), wr("cvp", 0, C), ALU.add)
-        ts(B("posW"), B("p3"), 0.5, ALU.mult, FP, ALU.add)
+        tt(B("p2"), B("p1"), B("iW"), ALU.min)
+        tt(B("p3"), B("p2"), wr("u2", 0, C), ALU.subtract)
+        tt(B("p1"), B("p3"), wr("u2", 0, C), ALU.max)
+        ts(B("posW"), B("p1"), 0.5, ALU.mult, FQ, ALU.add)
         scatter(B("R2"), B("posW"), B("iot"))
         e_plane(3)
         for lo, hi, tw in pieces:
@@ -403,7 +407,10 @@ def rank_program(g, core, T, topo):
         for b in range(4):
             mm(2 + b, 128, "qe", "se", 128 * b, "lq%d" % t, "ls%d" % t, 0, arr=arr_c)
         for b in range(4):
-            act(B("X", 4 * ST + b, 4 * C, 4), bank(2 + b, 128), AF.Copy)
+            if t == R - 1 and b % 2:
+                cp(B("X", 4 * ST + b, 4 * C, 4), bank(2 + b, 128))
+            else:
+                act(B("X", 4 * ST + b, 4 * C, 4), bank(2 + b, 128), AF.Copy)
 
     scores(0, ST, (0, 6))
     scores(ST, C, (1, 7))

from concourse.mybir import dt, AluOpType as ALU, AxisListType as AX, ActivationFunctionType as AF

C, M, LV2, ST, R = 448, 224, 128, 320, 3
STEP = (1, 2, 3)
PW = 240
UW = 256
C2 = 2 * C
BIG = 2.0 ** 21
HUGE = 2.0 ** 80
TINY = 2.0 ** -120
BY_SCAN = (2, 3)
F32, BF, I32, U16, Q4, U8 = "float32", "bfloat16", "int32", "uint16", "float8_e4m3fn_x4", "uint8"

SCRATCH = {}
for _n, _w, _d in [
    ("X", 4 * C, BF), ("XH", 4 * C2, BF), ("E", 4 * C2, BF), ("ut", 512, BF), ("vt", 512, BF), ("Z", 4 * PW, BF), ("U", 8 * UW, BF), ("H", 4 * PW, BF),
    ("Lt", 512, BF), ("eb", 2048, BF), ("ones", 512, BF), ("zeros", M, BF), ("alt", C2, BF),
    ("qx", C, Q4), ("sx", C, U8), ("qu", 128, Q4), ("su", 128, U8), ("qur", 128, Q4), ("sur", 128, U8), ("qv", 128, Q4), ("sv", 128, U8),
    ("qw", 512, Q4), ("sw", 512, U8), ("qe", 512, Q4), ("se", 512, U8), ("qz", PW, Q4), ("sz", PW, U8),
    ("iot", C, F32), ("iott", 2 * C, F32), ("K", C, F32), ("Kb", C, BF), ("j16", 16, F32), ("k16", 64, F32), ("qo", 28, U16), ("iW", 28, F32),
    ("dm", M, F32), ("keep", M, F32), ("m01", 32, F32), ("mbig", 32, F32), ("j2", 32, F32),
    ("pi", 8, I32), ("pf", 4, F32), ("fx", 16, F32), ("ui", 8, I32), ("uo", 8, U16), ("twi", 28, I32), ("tw0", 28, U16),
    ("S", C, F32), ("S2", C, F32), ("d", C2, F32), ("thr0", C2, F32), ("thr1", C2, F32), ("un", C, BF), ("c2", C, BF), ("K4", C, BF), ("kt", C, BF),
    ("cvb", C, BF), ("cvk", C, BF), ("cvt", C, BF), ("w1", 28, F32), ("w2", 28, F32), ("w3", 28, F32),
    ("destW", 28, U16), ("kW", 28, U16), ("cW", 28, U16), ("R1", 512 + 2 * PW, F32), ("cvo", PW, F32), ("cvq", PW, F32),
    ("oW", 16, U16), ("vW", 16, U16), ("bR", PW, BF), ("cvz", PW, BF), ("bW", 16, U16),
    ("dU", M, F32), ("dM", M, F32), ("dS", M, F32), ("junk", 26 * M, BF), ("Mw", 48, F32), ("lb", 16, F32), ("xB", 32, F32),
    ("r3", 4, F32), ("T3", 96, F32), ("T4", 96, F32), ("r4", 4, F32), ("tau", 4, F32),
    ("eq", M, BF), ("cum", M, BF), ("sg", M, BF), ("e1", M, BF), ("LV", PW, F32), ("sig", C, BF), ("cg", C, BF), ("u2", C, BF),
    ("a0", C, F32), ("p1", 28, F32), ("p2", 28, F32), ("p3", 28, F32), ("posW", 28, U16), ("R2", C, F32), ("cvr", C, F32), ("pW", 28, U16),
    ("pt", C2, F32), ("pu", C2, F32), ("ptp", C, F32), ("cvn", C, F32), ("twS", 20, U16), ("yo", C, F32), ("oto", C, F32),
]:
    SCRATCH[_n] = ("sbuf", [128, _w], _d)
for _t in range(R):
    for _n, _w, _d in [("ql", 128, Q4), ("sl", 128, U8), ("nl", 8, U16), ("lq", 128, Q4), ("ls", 128, U8), ("ln", 8, U16)]:
        SCRATCH["%s%d" % (_n, _t)] = ("sbuf", [128, _w], _d)
SCRATCH["ps"] = ("psum", [128, 512 * 8], F32)

SEMAPHORES = ["cV", "cA", "cT", "cG", "sent"] + ["arrL%d" % t for t in range(R)] + ["arrC%d" % t for t in range(R)] + ["dm%d" % k for k in range(24)]

ORDER = {
    "V": "5 11 0-2 10 4 3 17 13 8-9 7 6 12 24 28 26 25 29 27 32 30-31 33-35 21 36-38 16 39-44 22 46 45 23 110 56 20 52 57 47 58 53 51 49 109 48 18 50 54-55 60 14 19 63 62 61 64 67 69 68 71 70 73 72 74 59 75-78 65 79 66 80-81 85 93 83 82 86 84 88 87 89-92 94-96 98 97 99-100 103-105 101 106 108 107 102 111-113 115 114 116-123 136 125 135 124 137 15 138-139 131 141 140 132 126 142-146 129 147 127 148-149 133 130 150 161 134 128 155 152 156 154 153 151 157 159 158 166 165 164 163 160 167 170-171 173 172 175 174 177 176 162 178-182 168 183 169 184-185 189 197 187 186 190 188 192-194 191 195-196 198-204 207-210 212 211 205 213 206 214-227 238 237 228 239 233 240-244 261 245 235 234 246 232 247 263 248-249 251 230 250 231 252 236 256 262 254 229 253 255 259 257 260 258 265-269 272-273 275 274 277 276 279 278 264 280-284 270 285 271 286-287 291 299 289 288 292 290 294-298 300-301 303-304 306 302 305 309 307-308 293 310-315 317 316",
    "A": "1 0 3 25 4 26 10 2 18 24 6 13 22 21 16-17 5 28 35 14 27 34 30 19 29 15 33 8 32 7 36 31 11 20 23 9 12 37 42 40 39 41 38 45 44 57-58 47 56 48 46 50 54 49 55 52-53 43 51 61 65 63 59 64 71 60 66-67 62 74 68 72 69-70 75 73 77 76 79 78 80-93 95 97 109 98 94 102 100 103 99 105 96 108 110 113 115 114 112 111 123 107 130-131 106 117 104 124 129 120 128 126 125 118 121 127 122 116 101 119 132 136 133 138 137 134 139 144 140 147 141 135 145 143 142 148 146 149 151-154 150 156-158 155 159-161 164 163 162 165-168 173 169 184 170-171 176 181 175 179 182 180 174 172 190 188 187 189 186 185 178 205-206 192 191 183 200 194 197 201 204 193 195 202 198 177 203 196 199 207 211 213 212 208 214 219 215 209 222 210 216 220 217-218 223 221 229 228 225 224 230-232 227 226 233 235-236 234 240 238-239 237",
    "T": "3 0-2 5-6 4 7-15 18 17 16 19-20 23 22 21 24-26 28-29 27 30 32 31 33-35",
    "G": "3 1 0 2 4 8 12 10 6 5 11 7 9 13-15 18 22-23 16 19 21 20 17 24-25 29 28 26 30-31 34 27 33 32 35-37",
    "Y": "0-4 6 5 7-9",
}


def rank_program(g, core, T, topo):
    rank = T.rank_of(core)
    if rank is None:
        return
    n_ranks = len(T.cores)
    queue = {"V": g.vector, "A": g.scalar, "T": g.tensor, "G": g, "Y": g.sync}
    ops = []
    seen = {}
    n_dma = [0]

    def ap(v):
        return T[v[0]][:, v[1]:v[2]:v[3]] if v[3] != 1 else T[v[0]][:, v[1]:v[2]]

    def B(name, lo=0, hi=None, step=1):
        return (name, lo, SCRATCH[name][1][1] if hi is None else hi, step)

    def col(name, c):
        return (name, c, c + 1, 1)

    def add(q, emit, reads, writes, stream=None, arrivals=()):
        acc = []
        for vs, w in ((reads, False), (writes, True)):
            for v in vs:
                if v[0] == "ps":
                    acc.append(("ps", v[1] // 512 * 512, v[1] // 512 * 512 + 512, 1, True))
                else:
                    acc.append((v[0], v[1], v[2], v[3], w))
        deps = set()
        for n, lo, hi, st, w in acc:
            for l2, h2, s2, w2, k in seen.get(n, ()):
                if lo < h2 and l2 < hi and (w or w2) and not (st == s2 and (lo - l2) % st):
                    deps.add(k)
        ops.append((q, emit, deps, stream or "c" + q, arrivals))
        for n, lo, hi, st, w in acc:
            lst = seen.setdefault(n, [])
            if w:
                lst[:] = [e for e in lst if not (lo <= e[0] and e[1] <= hi and (st == 1 or (st == e[2] and (lo - e[0]) % st == 0)))]
            lst.append((lo, hi, st, w, len(ops) - 1))

    def src(v):
        if len(v) == 2:
            return ap(v[0]).indirect(ap(v[1])), [v[0], v[1]]
        return ap(v), [v]

    def sc(s):
        return (ap(s), [s]) if isinstance(s, tuple) else (s, [])

    def ts(out, in0, s1, op0, s2=None, op1=None):
        a, r = src(in0)
        b, r1 = sc(s1)
        c, r2 = sc(s2)
        if op1 is None:
            add("V", lambda: g.vector.tensor_scalar(ap(out), a, b, None, op0), r + r1, [out])
        else:
            add("V", lambda: g.vector.tensor_scalar(ap(out), a, b, c, op0, op1), r + r1 + r2, [out])

    def tt(out, in0, in1, op, arr=()):
        a, r = src(in0)
        add("V", lambda: g.vector.tensor_tensor(ap(out), a, ap(in1), op), r + [in1], [out], arrivals=arr)

    def cp(out, in_, arr=()):
        a, r = src(in_)
        add("V", lambda: g.vector.tensor_copy(ap(out), a), r, [out], arrivals=arr)

    def scatter(win, off, in_):
        add("V", lambda: g.vector.tensor_copy(ap(win).indirect(ap(off)), ap(in_)), [off, in_], [win])

    def scan(out, d0, d1, init, op0, op1):
        b, r = sc(init)
        add("V", lambda: g.vector.tensor_tensor_scan(ap(out), ap(d0), ap(d1), b, op0, op1), [d0, d1] + r, [out])

    def red(out, in_, op):
        add("V", lambda: g.vector.tensor_reduce(ap(out), ap(in_), AX.X, op), [in_], [out])

    def fill(out, c):
        add("V", lambda: g.vector.memset(ap(out), c), [], [out])

    def act(out, in_, func, bias=None, scale=None, accum=None, arr=()):
        a, r = src(in_)
        kw = {}
        for k, s in (("bias", bias), ("scale", scale)):
            if s is not None:
                kw[k], r1 = sc(s)
                r = r + r1
        if accum is not None:
            kw["accum_out"] = ap(accum)
        add("A", lambda: g.scalar.activation(ap(out), a, func, **kw), r, [out] + ([accum] if accum else []), arrivals=arr)

    def pool_copy(out, in_, n):
        add("G", lambda: g.affine_select(ap(out), ap(in_), [[0, n]], ALU.is_equal, 0.0, 0, 0), [in_], [out])

    def quant(qn, sn, lo, hi, tile, t0):
        t = B(tile, 4 * t0, 4 * (t0 + hi - lo))
        add("V", lambda: g.vector.quantize_mx(ap(B(qn, lo, hi)), ap(B(sn, lo, hi)), ap(t)), [t], [B(qn, lo, hi), B(sn, lo, hi)])

    def bank(k, n):
        return B("ps", 512 * k, 512 * k + n)

    def mm(k, n, wq, ws, w0, xq, xs, x0, arr=()):
        o = bank(k, n)
        r = [B(wq, w0, w0 + 128), B(ws, w0, w0 + 128), B(xq, x0, x0 + n), B(xs, x0, x0 + n)]
        add("T", lambda: g.tensor.matmul_mx(ap(o), ap(r[0]), ap(r[1]), ap(r[2]), ap(r[3]), True, True), r, [o], arrivals=arr)

    def dma(q, out, in_, reads, writes):
        s = "dm%d" % n_dma[0]
        n_dma[0] += 1
        add(q, lambda: queue[q].dma_start(out, in_), reads, writes, stream=s)

    def iota(out, pattern, base, cm):
        if SCRATCH[out[0]][2] == I32:
            add("G", lambda: g.iota(ap(out), pattern, base, cm), [], [out])
        else:
            add("G", lambda: g.iota(ap(out), pattern, base, cm, allow_small_or_imprecise_dtypes=True), [], [out])

    def conv(out, in_, n, k="K"):
        scan(out, B(k, 0, n), in_, 0.0, ALU.add, ALU.min)

    def wr(name, lo, hi):
        return B(name, lo + 15, hi, 16)

    def pair(name, half, lo=0, hi=C, plane=0):
        return B(name, C2 * plane + 2 * lo + half, C2 * plane + 2 * hi, 2)

    def plane(name, p):
        return B(name, C2 * p, C2 * p + C2)

    fixes = [(BIG, 0.0), (-512.0, 1.0), (1024.0, 0.0), (512.0, 0.0), (256.0, 0.0), (BIG / 2, -1.0), (-BIG, 0.0), (2 * BIG, 0.0), (2 * BIG, 1.0),
             (8192.0, -1537.0), (2044.0, 0.0), (512.0, 1.0), (-9216.0, 2048.0), (256.0, -1.0)]
    FI, FM, F2, F1, FC, FP, FN, FE, FO, FT, FU, FD, FS, FQ = [col("fx", k) for k in range(14)]

    dma("Y", ap(B("X", 0, 4 * ST)), T.x[:, 0:4 * ST], [], [B("X", 0, 4 * ST)])
    dma("A", ap(B("ut")), T.u[:, :], [], [B("ut")])
    dma("A", ap(B("X", 4 * ST, 4 * C)), T.x[:, 4 * ST:4 * C], [], [B("X", 4 * ST, 4 * C)])
    dma("Y", ap(B("twi")), T.tw[:, :], [], [B("twi")])
    dma("Y", ap(B("qw")).bitcast(dt.uint8), T.wc[:, :], [B("X"), B("ut")], [B("qw")])
    dma("Y", ap(B("sw")), T.ws[:, :], [], [B("sw")])
    dma("Y", ap(B("vt")), T.v[:, :], [], [B("vt")])

    iota(B("pi", 0, 4), [[1, 2], [0, 2]], 0, 1)
    iota(B("j16"), [[1, 16]], 0, 0)
    iota(B("ui"), [[16, 8]], 0, 0)
    iota(B("iot"), [[1, C]], 0, 0)
    iota(B("j2"), [[1, 2], [0, 16]], 0, 0)
    fill(B("zeros"), 0.0)
    ts(B("pi", 5, 7), B("pi", 1, 3), 15, ALU.bitwise_and)
    ts(B("pi", 4, 5), B("pi", 0, 1), 4, ALU.logical_shift_right, 1, ALU.bitwise_and)
    fill(B("ones"), 1.0)
    cp(B("pf", 0, 3), B("pi", 4, 7))
    fill(B("R1"), 0.0)
    ts(col("pf", 3), col("pf", 1), 15.0, ALU.not_equal)
    ts(B("qo"), B("zeros", 0, 28), col("pf", 1), ALU.add)
    ts(B("k16", 16, 32), B("j16"), col("pf", 1), ALU.is_equal, 2 * BIG, ALU.mult)
    ts(B("k16", 32, 48), B("j16"), col("pf", 2), ALU.is_equal, -BIG, ALU.mult)
    ts(B("k16", 48, 64), B("j16"), 0.0, ALU.not_equal)
    fill(B("U", 0, 4 * UW), 0.0)
    tt(B("k16", 0, 16), B("k16", 16, 32), B("k16", 32, 48), ALU.add)
    cp(B("uo"), B("ui"))
    fill(B("LV"), 0.0)
    fill(B("Mw", 16, 32), 0.0)
    fill(B("H"), 0.0)
    fill(pair("alt", 0), 0.0)
    fill(pair("alt", 1), 1.0)
    ts(B("m01"), B("j2"), col("pf", 0), ALU.is_equal)
    ts(B("mbig"), B("j2"), col("pf", 0), ALU.not_equal, 1024 * HUGE, ALU.mult)
    ts(B("p1"), B("iot", 0, C, 16), col("pf", 1), ALU.add)
    ts(B("p2"), B("p1"), 2.0, ALU.mult, 2.0 * (LV2 + 1), ALU.add)
    act(B("K"), (B("k16", 0, 16), B("qo")), AF.Copy)
    act(B("iott", 0, C), B("iot"), AF.Copy, scale=TINY)
    act(B("iott", C, 2 * C), B("iot"), AF.Copy, scale=TINY)
    act(B("Kb"), B("K"), AF.Copy, scale=512.0 / BIG)
    act(B("K4"), B("K"), AF.Copy, scale=4.0 / BIG)
    for k, (a, b) in enumerate(fixes):
        act(col("fx", k), col("pf", 3), AF.Identity, bias=b, scale=a)

    ts(B("iW"), B("p2"), F2, ALU.subtract)
    quant("qu", "su", 0, 128, "ut", 0)
    add("V", lambda: g.vector.tensor_copy(ap(B("qur")).bitcast(dt.uint32), ap(B("qu")).bitcast(dt.uint32).indirect(ap(B("uo")))), [B("qu"), B("uo")], [B("qur")])
    add("V", lambda: g.vector.tensor_copy(ap(B("sur")), ap(B("su")).indirect(ap(B("uo")))), [B("su"), B("uo")], [B("sur")])

    def scores(lo, hi, banks):
        quant("qx", "sx", lo, hi, "X", lo)
        for k in banks:
            mm(k, hi - lo, "qur", "sur", 0, "qx", "sx", lo)
        if banks:
            act(B("S", lo, hi), bank(banks[-1], hi - lo), AF.Copy)

    def planes(lo, hi):
        for p in range(4):
            pool_copy(pair("XH", 0, lo, hi, p), B("X", 4 * lo + p, 4 * hi, 4), hi - lo)

    def ties(thr, lo, hi, tw, arr=()):
        tt(pair(thr, 1, lo, hi), (B("iott", lo, hi), tw), B("iott", C + lo, C + hi), ALU.subtract, arr=arr)

    def under_a(thr, lo, hi, tw):
        n, a, b = hi - lo, lo // 16, hi // 16
        d = pair("d", 0, lo, hi)
        if lo:
            tt(d, B("S2", lo, hi), bank(1, n), ALU.subtract)
        else:
            tt(d, (B("S", lo, hi), tw), B("S2", lo, hi), ALU.subtract)
        tt(B("un", lo, hi), d, pair(thr, 1, lo, hi), ALU.is_gt)
        scan(B("c2", lo, hi), B("un", lo, hi), B("un", lo, hi), col("c2", lo - 1) if lo else 2.0, ALU.add, ALU.add)
        act(B("kt", lo, hi), (B("c2", lo, hi), tw), AF.Copy)
        conv(B("cvk", lo, hi), B("un", lo, hi), n, "K4")
        conv(B("cvb", lo, hi), B("c2", lo, hi), n, "Kb")
        ts(B("p3", a, b), wr("cvk", lo, hi), 2048.0, ALU.mult, FT, ALU.add)
        tt(B("w1", a, b), wr("cvb", lo, hi), B("p3", a, b), ALU.add)
        conv(B("cvt", lo, hi), B("kt", lo, hi), n, "Kb")
        tt(B("w2", a, b), wr("cvt", lo, hi), B("w1", a, b), ALU.max)
        ts(B("destW", a, b), B("w2", a, b), FD, ALU.add)

    def under_b(lo, hi):
        scatter(B("R1"), B("destW", lo // 16, hi // 16), B("iot", lo, hi))

    def rank_part(k0, k1):
        a, b, n = k0 // 16, k1 // 16, k1 - k0
        top = C if k1 == M else ST
        conv(B("cvo", k0, k1), B("R1", 516 + 2 * k0, 516 + 2 * k1, 2), n)
        conv(B("cvq", k0, k1), B("R1", 5 + 2 * k0, 4 + 2 * k1, 2), n)
        ts(B("oW", a, b), wr("cvo", k0, k1), 2.0, ALU.mult, FE, ALU.add)
        ts(B("vW", a, b), wr("cvq", k0, k1), FI, ALU.add)
        act(B("dU", k0, k1), (B("d", 0, 2 * top), B("oW", a, b)), AF.Copy)
        act(B("bR", k0, k1), (B("c2", 0, top), B("vW", a, b)), AF.Copy)
        for p in range(4):
            u1 = B("U", UW * p + 2 + k0, UW * p + 2 + k1)
            act(u1, (B("XH", C2 * p, C2 * p + 2 * top), B("oW", a, b)), AF.Copy, scale=0.5)
            cp(B("U", UW * (4 + p) + 2 + k0, UW * (4 + p) + 2 + k1), u1)
        scan(B("dM", k0, k1), B("dU", k0, k1), B("dm", k0, k1), 0.0, ALU.max, ALU.min)
        scan(B("dS", k0, k1), B("keep", k0, k1), B("dM", k0, k1), 0.0, ALU.mult, ALU.add)
        conv(B("cvz", k0, k1), B("bR", k0, k1), n, "Kb")
        ts(B("bW", a, b), wr("cvz", k0, k1), 0.5, ALU.mult, FC, ALU.add)
        for c in range(b):
            lo, j = (k0, 16) if c < a else (0, 0)
            o = M * (c + j)
            act(B("junk", o + lo, o + k1), B("dU", lo, k1), AF.Sign, bias=col("dS", 16 * c + 15), scale=-1.0, accum=col("Mw", c + j))

    def e_plane(p):
        h = (B("H", PW * p, PW * p + PW), B("cW"))
        if p in BY_SCAN:
            act(pair("XH", 1, 0, C, p), h, AF.Copy)
            scan(plane("E", p), B("alt"), plane("XH", p), 0.0, ALU.mult, ALU.add)
        else:
            tt(pair("E", 1, 0, C, p), h, B("X", p, 4 * C, 4), ALU.add)

    def h_plane(b):
        act(col("H", PW * b + 1), B("ps", 512 * (2 + b) + M - 1, 512 * (2 + b) + M), AF.Copy, scale=0.03125)
        act(B("H", PW * b + 2, PW * b + M + 2), bank(2 + b, M), AF.Copy, scale=0.03125)

    def middle(t, pieces):
        rank_part(ST // 2 if t else 0, M)
        du = B("dU")
        act(B("U", 1, 4 * UW, UW), B("U", M + 1, 4 * UW, UW), AF.Copy)
        act(B("U", 4 * UW + 1, 8 * UW, UW), B("U", M + 1, 4 * UW, UW), AF.Copy)
        ts(B("p2"), wr("cvk", 0, C), 511.0, ALU.mult, FU, ALU.add)
        tt(B("w3"), B("w2"), B("p2"), ALU.subtract)
        ts(B("cW"), wr("cvb", 0, C), 0.5, ALU.mult, FC, ALU.add)
        ts(B("kW"), B("w3"), 0.5, ALU.mult, FC, ALU.add)
        for p in range(4):
            a2 = UW * (4 + p)
            tt(B("Z", p, 4 * M, 4), (B("U", UW * p, UW * p + PW), B("bW", 0, 14)), B("U", a2 + 1, a2 + 1 + M), ALU.add)
        quant("qz", "sz", 0, M, "Z", 0)
        for b in range(4):
            mm(2 + b, M, "qw", "sw", 128 * b, "qz", "sz", 0)
        h_plane(0)
        h_plane(1)
        e_plane(0)
        e_plane(1)
        if t:
            tt(B("Mw", 32, 46), B("Mw", 0, 14), B("Mw", 16, 30), ALU.add)
        mw, dw, xb, xa = B("Mw", 32, 46) if t else B("Mw", 0, 14), wr("dS", 0, M), B("xB", 0, 14), B("xB", 16, 30)
        act(B("junk", 14 * M, 14 * M + 14), mw, AF.Sign, bias=-96.5, scale=-1.0, accum=col("r3", 2))
        ts(B("lb", 0, 14), mw, -96.5, ALU.is_le, HUGE, ALU.mult)
        act(B("T3", 64, 96), B("m01"), AF.Identity, scale=col("r3", 2))
        h_plane(2)
        tt(xb, dw, B("lb", 0, 14), ALU.add)
        tt(xa, dw, B("lb", 0, 14), ALU.min)
        red(col("r3", 0), xb, ALU.min)
        red(col("r3", 1), xa, ALU.max)
        ts(B("T3", 0, 32), B("mbig"), col("r3", 0), ALU.add)
        ts(B("T3", 32, 64), B("m01"), col("r3", 1), ALU.mult)
        add("V", lambda: g.vector.transpose(ap(B("T4")), ap(B("T3"))), [B("T3")], [B("T4")])
        act(B("T3", 64, 96), B("T4", 64, 96), AF.Identity, accum=col("r4", 2))
        red(col("r4", 0), B("T4", 0, 32), ALU.min)
        red(col("r4", 1), B("T4", 32, 64), ALU.max)
        ts(col("tau", 0), col("r4", 2), -97.0, ALU.is_lt, col("r4", 0), ALU.mult)
        ts(col("tau", 1), col("tau", 0), col("r4", 1), ALU.max)
        tau = col("tau", 1)
        act(B("sg"), du, AF.Sign, bias=tau, scale=-1.0)
        ts(B("eq"), du, tau, ALU.is_equal, 1.0 / 256, ALU.mult)
        act(B("junk", 15 * M, 16 * M), B("sg"), AF.Relu, scale=1.0 / 256, accum=col("tau", 2))
        act(B("e1"), B("sg"), AF.Identity, bias=1.0)
        h_plane(3)
        scan(B("cum"), B("zeros"), B("eq"), col("tau", 2), ALU.add, ALU.add)
        scan(B("LV", 2, 2 + M), B("cum"), B("e1"), -4.0, ALU.max, ALU.subtract)
        act(B("sig"), (B("LV"), B("kW")), AF.Sign, bias=64.5 / 256 - 1, scale=-1.0)
        scan(B("cg"), B("sig"), B("ones", 0, C), 0.0, ALU.add, ALU.add)
        conv(B("cvb"), B("sig"), C, "K4")
        conv(B("u2"), B("cg"), C, "Kb")
        e_plane(2)
        ts(B("p1"), wr("cvb", 0, C), -2048.0, ALU.mult, FS, ALU.add)
        scan(B("a0"), B("ones", 0, C), B("sig"), 0.0, ALU.add, ALU.subtract)
        tt(B("p2"), B("p1"), B("iW"), ALU.min)
        tt(B("p3"), B("p2"), wr("u2", 0, C), ALU.subtract)
        tt(B("p1"), B("p3"), wr("u2", 0, C), ALU.max)
        ts(B("posW"), B("p1"), 0.5, ALU.mult, FQ, ALU.add)
        scatter(B("R2"), B("posW"), B("iot"))
        e_plane(3)
        for lo, hi, tw in pieces:
            act(pair("pt", 1, lo, hi), (B("cg", lo, hi), tw), AF.Copy)
        for lo, hi, tw in pieces:
            act(pair("pu", 1, lo, hi), (B("a0", lo, hi), tw), AF.Copy)
        conv(B("cvr", 0, LV2), B("R2", 0, LV2), LV2)

    def remote(out, in_, reads, sem, dst, mask):
        rid, pid, _ = topo.addr(dst)
        add("G", lambda: g.remote_dma(out, in_, T.sem[sem], T.sem.sent, pid, rid, mask), reads, [], stream="remote")

    sent = [0]

    def send(t):
        dst = T.cores[(rank + STEP[t]) % n_ranks]
        eng = topo.engines(core, dst)
        half = len(eng) // 2
        masks = [sum(1 << e for e in es) for es in (eng, eng[:half], eng[half:])]
        ls = B("pW", 0, 8)
        ts(ls, wr("cvr", 0, LV2), 2.0, ALU.mult, FO, ALU.add)
        conv(B("cvr", LV2, C), B("R2", LV2, C), ST)
        for p in range(2):
            act(B("Lt", p, 512, 4), (plane("E", p), ls), AF.Copy)
            cp(B("Lt", 2 + p, 512, 4), (plane("E", 2 + p), ls))
        act(B("ptp", 0, LV2), (B("pt"), ls), AF.Copy)
        ts(B("pW", 8, 28), wr("cvr", LV2, C), 2.0, ALU.mult, FO, ALU.add)
        quant("ql%d" % t, "sl%d" % t, 0, 128, "Lt", 0)
        remote(ap(B("lq%d" % t)).bitcast(dt.uint8), ap(B("ql%d" % t)).bitcast(dt.uint8), [B("ql%d" % t)], "arrC%d" % t, dst, masks[1])
        remote(ap(B("ls%d" % t)), ap(B("sl%d" % t)), [B("sl%d" % t)], "arrC%d" % t, dst, masks[2])
        conv(B("cvn", 0, LV2), B("ptp", 0, LV2), LV2)
        ts(B("nl%d" % t), wr("cvn", 0, LV2), 0.5, ALU.mult, FP, ALU.add)
        remote(ap(B("ln%d" % t)), ap(B("nl%d" % t)), [B("nl%d" % t)], "arrL%d" % t, dst, masks[0])
        sent[0] += len(eng) + 2 * half
        back = topo.engines(T.cores[(rank - STEP[t]) % n_ranks], core)
        return [("arrL%d" % t, len(back))], [("arrC%d" % t, len(back) // 2 * 2)]

    def stay(thr_old, thr_new):
        qs = B("pW", 8, 28)
        for p in range(2):
            act(B("X", p, 4 * ST, 4), (plane("E", p), qs), AF.Copy)
            cp(B("X", 2 + p, 4 * ST, 4), (plane("E", 2 + p), qs))
        act(B("ptp", LV2, C), (B("pu"), qs), AF.Copy)
        scores(0, ST, (6, 0) if thr_new else ())
        if thr_new:
            planes(0, ST)
            conv(B("cvn", LV2, C), B("ptp", LV2, C), ST)
            ts(B("twS"), wr("cvn", LV2, C), 0.5, ALU.mult, FP, ALU.add)
            cp(B("S2", 0, ST), bank(6, ST))
            act(pair(thr_new, 1, 0, ST), (B(thr_old), qs), AF.Copy)

    def unpack(t, arr_c):
        for b in range(4):
            mm(2 + b, 128, "qe", "se", 128 * b, "lq%d" % t, "ls%d" % t, 0, arr=arr_c)
        for b in range(4):
            if t == R - 1 and b % 2:
                cp(B("X", 4 * ST + b, 4 * C, 4), bank(2 + b, 128))
            else:
                act(B("X", 4 * ST + b, 4 * C, 4), bank(2 + b, 128), AF.Copy)

    scores(0, ST, (0, 6))
    scores(ST, C, (1, 7))
    planes(0, C)
    cp(B("tw0"), B("twi"))
    cp(B("S2", 0, ST), bank(0, ST))
    cp(B("S2", ST, C), bank(1, LV2))
    ties("thr0", 0, C, B("tw0"))
    act(B("dm"), (B("k16", 16, 32), B("qo", 0, 14)), AF.Copy, scale=HUGE / (2 * BIG))
    act(B("keep"), (B("k16", 48, 64), B("qo", 0, 14)), AF.Copy)
    for p in range(4):
        act(pair("XH", 1, 0, C, p), B("iot"), AF.Copy)
    act(pair("d", 1), B("iot"), AF.Copy)
    under_a("thr0", 0, C, B("tw0"))
    for name, half in (("thr0", 0), ("thr1", 0), ("pt", 0), ("pu", 0)):
        act(pair(name, half), B("iot"), AF.Copy)
    for p in range(4):
        if p not in BY_SCAN:
            act(pair("E", 0, 0, C, p), B("iot"), AF.Copy)
    under_b(0, C)
    for b in range(4):
        o = B("eb", 512 * b, 512 * b + 512)
        add("G", lambda o=o, b=b: g.affine_select(ap(o), ap(B("ones")), [[-1, 512]], ALU.is_equal, 0.0, b, 4), [B("ones")], [o])
    pieces = [(0, C, B("tw0"))]
    for t in range(R):
        middle(t, pieces)
        arr_l, arr_c = send(t)
        last = t == R - 1
        old, new = "thr%d" % (t % 2), "thr%d" % (1 - t % 2)
        stay(old, None if last else new)
        if t == 0:
            quant("qe", "se", 0, 512, "eb", 0)
            quant("qv", "sv", 0, 128, "vt", 0)
        twa = B("ln%d" % t)
        if last:
            break
        under_a(new, 0, ST, B("twS"))
        unpack(t, arr_c)
        scores(ST, C, (1,))
        planes(ST, C)
        act(B("S2", ST, C), (B("S", ST, C), twa), AF.Copy, arr=arr_l)
        under_b(0, ST)
        rank_part(0, ST // 2)
        ties(new, ST, C, twa, arr=arr_l)
        under_a(new, ST, C, twa)
        under_b(ST, C)
        pieces = [(0, ST, B("twS")), (ST, C, twa)]

    def finish(lo, hi, k):
        mm(k, hi - lo, "qv", "sv", 0, "qx", "sx", lo)
        dma("Y", T.oc[:, 4 * lo:4 * hi], ap(B("qx", lo, hi)).bitcast(dt.uint8), [B("qx", lo, hi)], [])
        cp(B("yo", lo, hi), bank(k, hi - lo))
        dma("Y", T.y[:, lo:hi], ap(B("yo", lo, hi)), [B("yo", lo, hi)], [])

    finish(0, ST, 0)
    act(B("oto", 0, ST), B("ptp", LV2, C), AF.Identity, bias=-1.0, scale=0.5)
    unpack(R - 1, arr_c)
    scores(ST, C, ())
    finish(ST, C, 1)
    for k in range(4):
        dma("A", T.osc[4 * k:4 * k + 4, :], T.sx[32 * k:32 * k + 4, :], [B("sx")], [])
    cp(B("oto", ST, C), (B("iot", ST, C), twa), arr=arr_l)
    dma("Y", T.ot[:, :], T.oto[0:128:16, :], [B("oto")], [])

    order = list(range(len(ops)))
    if ORDER:
        line = {}
        for q in queue:
            mine = [k for k in order if ops[k][0] == q]
            runs = [[int(x) for x in w.split("-")] for w in ORDER[q].split()]
            line[q] = [mine[i] for r in runs for i in range(r[0], r[-1] + 1)][::-1]
            assert sorted(line[q]) == mine
        order, done = [], set()
        while len(order) < len(ops):
            k = [line[q].pop() for q in queue if line[q] and ops[line[q][-1]][2] <= done][:]
            assert k
            order += k
            done |= set(k)
    known = {q: {} for q in queue}
    clock, token, place, waits, needed = {}, {}, {}, {}, set()
    for k in order:
        q, emit, deps, stream, arrivals = ops[k]
        mine = known[q]
        waits[k] = []
        for j in sorted(deps, key=lambda j: -token[j][1]):
            s, p = token[j]
            if mine.get(s, 0) < p:
                waits[k].append(j)
                needed.add(j)
                mine[s] = p
                for s2, p2 in clock[j].items():
                    mine[s2] = max(mine.get(s2, 0), p2)
        for s, n in arrivals:
            if s not in mine:
                mine[s] = 1
                waits[k].append((s, n))
        place[stream] = place.get(stream, 0) + 1
        token[k] = (stream, place[stream])
        clock[k] = dict(mine)
    count, value = {}, {}
    for k in order:
        q, (s, p) = ops[k][0], token[k]
        for w in waits[k]:
            if isinstance(w, tuple):
                queue[q].wait_ge(T.sem[w[0]], w[1])
            else:
                queue[q].wait_ge(T.sem[token[w][0]], value[w])
        ins = ops[k][1]()
        if s != "remote" and (k in needed or p == place[s]):
            n = 16 if s.startswith("dm") else 1
            ins.then_inc(T.sem[s], n)
            count[s] = count.get(s, 0) + n
            value[k] = count[s]
    for s, n in count.items():
        g.wait_ge(T.sem[s], n)
    g.wait_ge(T.sem.sent, sent[0])
